import numpy as np, ml_dtypes
CORES = [6,15,38,47]
N = 4
import mx_ref
BF = ml_dtypes.bfloat16
def pick(q, e):
    c = np.concatenate([q[0].reshape(128, -1, 4), np.zeros((128, 1, 4), np.uint8)], axis=1); s = np.concatenate([q[1], np.ones((16, 1), np.uint8)], axis=1)
    return (np.ascontiguousarray(c[:, e].reshape(128, -1)), np.ascontiguousarray(s[:, e]))
def join(*qs):
    return (np.concatenate([q[0] for q in qs], axis=1), np.concatenate([q[1] for q in qs], axis=1))
def put(q, e, v):
    c, s = q[0].reshape(128, -1, 4).copy(), q[1].copy(); c[:, e] = v[0].reshape(128, -1, 4); s[:, e] = v[1]
    return (c.reshape(128, -1), s)
def pk(c, s):
    return (np.ascontiguousarray(c), mx_ref.live(s))
def emit(q):
    return q[0], q[1]
def cols(t, e):
    v = np.concatenate([t.reshape(128, -1, 4), np.zeros((128, 1, 4), BF)], axis=1)
    return np.ascontiguousarray(v[:, e]).reshape(128, -1)
def cut(t, i, w=512):
    return t[:, w * i:w * i + w]
def decode(q):
    o = []
    for b in range(4):
        e = np.zeros((128, 128, 4), np.float32); e[np.arange(128), np.arange(128), b] = 1
        o.append(mx_ref.matmul(mx_ref.quantize(e.reshape(128, 512).astype(BF)), q))
    return np.stack(o, axis=2).reshape(128, -1)
def f(rng, *shape):
    return mx_ref.flush((rng.standard_normal(shape, dtype=np.float32) * np.exp2(rng.integers(-2, 3, shape[:-1] + (1,)))).astype(BF))
def wide(rng, *shape, cols=0):
    v = rng.standard_normal(shape, dtype=np.float32) * np.exp2(rng.integers(-12, 13, shape)).astype(np.float32)
    if cols: v *= np.repeat(np.exp2(rng.integers(-cols, cols + 1, shape[:-2] + (1, shape[-1] // 4))) * (rng.random(shape[:-2] + (1, shape[-1] // 4)) > 0.0625), 4, axis=-1).astype(np.float32)
    return mx_ref.flush(v.astype(BF))
G, T, CAPP, R = 32, 192, 64, 3
def fit(v):
    v = np.array(v, np.float32)
    v[np.abs(v) < np.float32(2.0 ** -10)] = 0
    return v.astype(BF)
def plain(rng):
    return {"cb": fit(f(rng, N, 128, 4 * G)), "x": fit(f(rng, N, 128, 4 * R * T)), "w": f(rng, N, 128, 512)}
def part(rng, lab, k):
    s = (128, len(k), 4)
    v = np.where(k[None, :, None] == 2, rng.standard_normal(s), 1 + rng.random(s))
    return (v * (lab[:, None] == k[None, :])[:, :, None]).reshape(128, -1)
def setup_inputs(rng):
    return plain(rng)
def setup_inputs_crowd(rng):
    d = plain(rng)
    lab = rng.permutation(np.repeat([0, 1, 2], [40, 40, 48]))
    q, g = int(rng.integers(0, N - 2)), rng.permutation(G)[:2]
    home = int(rng.integers(0, R))
    rush = (home + 1 + int(rng.integers(0, R - 1))) % R
    cb = np.stack([part(rng, lab, np.full(G, 2)) for r in range(N)])
    k, size = np.zeros(G, int), np.full(G, 2.0 ** -6)
    k[g[1]] = 1
    size[g] = 1
    cb[q] = part(rng, lab, k) * np.repeat(size, 4)
    kinds = np.full((N, R, T), 2)
    for t in range(R):
        three, whole = np.sort(rng.permutation(N)[:3]), -1
        if t == home: three = np.concatenate([[q], np.sort(q + 1 + rng.permutation(N - 1 - q)[:2])])
        if t == rush:
            four, j = np.sort(rng.permutation(N)[:4]), int(rng.integers(0, 3))
            three, whole = np.delete(four, j), int(four[j])
        for s in range(N):
            more = int(rng.integers(1, T // 8 + 1))
            if s == three[0]: e = np.concatenate([np.zeros(CAPP, int), np.ones(more, int)])
            elif s == three[1]: e = np.concatenate([np.zeros(CAPP - 1, int), np.ones(1, int)])
            elif s == three[2]: e = np.concatenate([np.zeros(CAPP - 1, int), np.ones(1, int), rng.integers(0, 2, more)])
            elif s == whole: e = np.concatenate([np.zeros(CAPP, int), np.ones(T - CAPP, int)])
            else: e = np.zeros(int(rng.integers(CAPP // 2, CAPP + T // 8 + 1)), int)
            kinds[s, t, np.sort(rng.permutation(T)[:len(e)])] = e
    d["cb"], d["x"] = fit(cb), fit(np.stack([part(rng, lab, kinds[s].reshape(-1)) for s in range(N)]))
    return d
def setup_inputs_ties(rng):
    d = plain(rng)
    H = G // 2
    shared = fit(rng.standard_normal((128, 4 * H)))
    for r in range(N):
        both = np.concatenate([shared, fit(rng.standard_normal((128, 4 * H)))], axis=1)
        d["cb"][r] = cols(both, rng.permutation(np.concatenate([rng.integers(0, H, G - H), H + np.arange(H)])))
        v = cut(d["x"][r], 0, 4 * T).copy().reshape(128, T, 4)
        at = rng.permutation(T)
        v[:, at[:H]] = shared.reshape(128, H, 4)
        v[:, at[H:H + T // 16]] = 0
        d["x"][r] = np.concatenate([cols(v.reshape(128, -1), rng.permutation(T)) for t in range(R)], axis=1)
    return d
def setup_inputs_full(rng):
    d = plain(rng)
    at = rng.permutation(128)
    own = at[None, :] == np.arange(128)[:, None]
    cb = (1 + rng.random((128, 128, 4))) * np.where(own, 1.0, 2.0 ** -8)[:, :, None]
    kinds, who = np.zeros((N, R, T), int), np.arange(128) // G
    least, below = [], []
    for t in range(R):
        s, q = [int(v) for v in rng.permutation(N)[:2]]
        mine, free = np.flatnonzero(who == q), np.flatnonzero(who != q)
        if t == 0 or t == R - 1:
            least.append(int(rng.choice([v for v in free if G <= v < 128 - G and v not in least])))
            free = free[free != least[-1]]
            below.append((s + 1 + int(rng.integers(0, N - 1))) % N)
        for r in range(N):
            if r == s: kinds[r, t] = rng.permutation(np.concatenate([mine, mine, rng.choice(free, T - 2 * G)]))
            elif r < s: kinds[r, t] = rng.choice(free, T)
            else: kinds[r, t] = rng.choice(np.concatenate([free, mine]), T)
    x = np.zeros((N, 128, R * T, 4))
    for r in range(N):
        k = kinds[r].reshape(-1)
        x[r] = np.where(own[:, k][:, :, None], 1 + rng.random((128, R * T, 4)), (2 * rng.random((128, R * T, 4)) - 1) * 2.0 ** -7)
    x[below[0]][:, :2] = -(1 + rng.random((128, 2, 4))) * np.where(own[:, least[0]], 2.0 ** -9, 2.0 ** -6)[:, None, None]
    size = np.where(own[:, least[1]], 2.0 ** 15, np.where(own[:, least[0]], 2.0 ** 24, 2.0 ** 21))
    i = (R - 1) * T
    x[below[1]][:, i:i + 2] = -(3 + rng.random((128, 2, 4))) * size[:, None, None]
    d["cb"] = fit(np.stack([cb[:, G * r:G * r + G].reshape(128, -1) for r in range(N)]))
    d["x"] = fit(x.reshape(N, 128, -1))
    return d
def setup_inputs_idle(rng):
    d = plain(rng)
    q, own = int(rng.integers(0, N)), rng.permutation(128) < 64
    cb = rng.standard_normal((N, 128, 4 * G))
    for r in range(N): cb[r] *= (own if r == q else ~own)[:, None]
    early = np.arange(4 * R * T) < 4 * (R - 1) * T
    d["cb"], d["x"] = fit(cb), fit(d["x"].astype(np.float32) * ~(own[:, None] & early[None, :]))
    return d
def setup_inputs_spread(rng):
    d = plain(rng)
    d["cb"] = fit(wide(rng, N, 128, 4 * G).astype(np.float32) * 64)
    d["x"] = fit(wide(rng, N, 128, 4 * R * T, cols=4).astype(np.float32) * 64)
    return d
def check_inputs(d):
    b = []
    for k, lo, hi in (("cb", -10, 28), ("x", -10, 28), ("w", -30, 30)):
        v = np.abs(d[k].astype(np.float32))
        if not (np.isfinite(v).all() and ((v == 0) | (v >= 2.0 ** lo) & (v <= 2.0 ** hi)).all()): b.append("a value of " + k)
    return b
def admitted(win):
    a = np.full((2, 128), -1)
    for s in range(N):
        n = np.zeros(N, int)
        for i in range(T):
            k = win[T * s + i]
            n[k // G] += 1
            if n[k // G] > CAPP: continue
            if a[0, k] < 0: a[0, k] = T * s + i
            elif a[1, k] < 0: a[1, k] = T * s + i
    return a
def reference(cb, x, w):
    y, ids = np.zeros((N, 128, R * 2 * G), np.float32), np.zeros((N, 1, R * 2 * G), np.float32)
    oc, osc = np.zeros((N, 128, 4 * G), np.uint8), np.zeros((N, 16, G), np.uint8)
    half, quarter = np.float32(0.5), np.float32(0.25)
    qw = [mx_ref.quantize(np.ascontiguousarray(w[r])) for r in range(N)]
    c = join(*[mx_ref.quantize(np.ascontiguousarray(cb[r])) for r in range(N)])
    for t in range(R):
        tok = join(*[mx_ref.quantize(np.ascontiguousarray(cut(x[s], t, 4 * T))) for s in range(N)])
        a = admitted(np.argmax(mx_ref.matmul(c, tok) + np.float32(0), axis=0))
        for r in range(N):
            e = a[:, G * r:G * r + G].T.reshape(-1)
            i = t * 2 * G
            y[r, :, i:i + 2 * G] = mx_ref.matmul(qw[r], pick(tok, e))
            ids[r, 0, i:i + 2 * G] = e
        v = decode(join(c, pick(tok, a[0]), pick(tok, a[1]))).reshape(128, 3, 128, 4)
        one = half * v[:, 0] + half * v[:, 1]
        two = half * v[:, 0] + (quarter * v[:, 1] + quarter * v[:, 2])
        new = np.where((a[1] >= 0)[None, :, None], two, one).reshape(128, 512).astype(BF)
        moved = np.flatnonzero(a[0] >= 0)
        c = put(c, moved, pick(mx_ref.quantize(np.ascontiguousarray(new)), moved))
    for r in range(N):
        oc[r], osc[r] = emit(pick(c, np.arange(G * r, G * r + G)))
    return {"y": y, "ids": ids, "oc": oc, "osc": osc}

@@ -1,0 +1,483 @@
+from concourse.bass import DstId, RemoteDMATransfer
+from concourse.mybir import dt, AluOpType as A, ActivationFunctionType as AF
+
+CODE = "float8_e4m3fn_x4"
+N, G, TOK, R, CAPP = 4, 32, 192, 3, 64
+BIG = 262144.0
+PEN = 524288.0
+FAR = 1.0e9
+LOW = -1.0e29
+
+SCRATCH = {
+    "cbt": ("sbuf", [128, 512], "bfloat16"), "xt": ("sbuf", [128, 2304], "bfloat16"), "wt": ("sbuf", [128, 512], "bfloat16"),
+    "zt": ("sbuf", [128, 1024], "bfloat16"), "pt": ("sbuf", [128, 528], "bfloat16"), "zz": ("sbuf", [128, 528], "bfloat16"),
+    "nt": ("sbuf", [128, 512], "bfloat16"), "ct": ("sbuf", [128, 2048], "bfloat16"), "et": ("sbuf", [128, 2048], "bfloat16"),
+    "cq": ("sbuf", [128, 512], CODE), "cqs": ("sbuf", [128, 512], "uint8"),
+    "eq": ("sbuf", [128, 512], CODE), "eqs": ("sbuf", [128, 512], "uint8"),
+    "cbq": ("sbuf", [128, 128], CODE), "cbs": ("sbuf", [128, 128], "uint8"),
+    "xq": ("sbuf", [128, 576], CODE), "xs": ("sbuf", [128, 576], "uint8"),
+    "wq": ("sbuf", [128, 128], CODE), "ws": ("sbuf", [128, 128], "uint8"),
+    "pq": ("sbuf", [128, 132], CODE), "pqs": ("sbuf", [128, 132], "uint8"),
+    "zq": ("sbuf", [128, 132], CODE), "zqs": ("sbuf", [128, 132], "uint8"),
+    "adm": ("sbuf", [128, 128], CODE), "adms": ("sbuf", [128, 128], "uint8"),
+    "rowi": ("sbuf", [128, 128], "float32"), "k16": ("sbuf", [128, 128], "float32"), "negc": ("sbuf", [128, 128], "float32"),
+    "ma": ("sbuf", [128, 128], "float32"), "mb": ("sbuf", [128, 128], "float32"), "msk": ("sbuf", [128, 128], "float32"),
+    "msk2": ("sbuf", [128, 128], "float32"), "ls1": ("sbuf", [128, 128], "float32"), "ls2": ("sbuf", [128, 128], "float32"),
+    "pcol": ("sbuf", [128, 1], "float32"), "pi": ("sbuf", [128, 1], "int32"), "qi": ("sbuf", [128, 1], "int32"),
+    "qcol": ("sbuf", [128, 1], "float32"), "qcol1": ("sbuf", [128, 1], "float32"), "corr": ("sbuf", [128, 1], "float32"),
+    "ncorr": ("sbuf", [128, 1], "float32"),
+    "ii": ("sbuf", [128, 16], "float32"), "tt": ("sbuf", [128, 16], "float32"), "lst": ("sbuf", [128, 16], "uint16"),
+    "offi": ("sbuf", [128, 32], "float32"), "pen": ("sbuf", [128, 32], "float32"), "cv": ("sbuf", [128, 32], "float32"),
+    "vv": ("sbuf", [128, 32], "float32"), "pm": ("sbuf", [128, 32], "float32"), "mx": ("sbuf", [128, 32], "float32"),
+    "sc": ("sbuf", [128, 32], "float32"), "rsa": ("sbuf", [128, 32], "float32"), "rsb": ("sbuf", [128, 32], "float32"),
+    "sz": ("sbuf", [128, 2], "float32"), "alst": ("sbuf", [128, 6], "uint16"), "mv": ("sbuf", [128, 2], "float32"),
+    "clst": ("sbuf", [128, 2], "uint16"), "ilst": ("sbuf", [128, 2], "uint16"), "gnew": ("sbuf", [128, 2], "float32"),
+    "s4": ("sbuf", [128, 128], "float32"), "hh": ("sbuf", [128, 128], "float32"), "hc": ("sbuf", [128, 128], "float32"),
+    "vi": ("sbuf", [128, 4], "int32"), "iv": ("sbuf", [128, 4], "int32"), "sv": ("sbuf", [128, 4], "int32"),
+    "s192": ("sbuf", [128, 4], "float32"), "idf": ("sbuf", [128, 4], "float32"), "val": ("sbuf", [128, 4], "float32"),
+    "idg": ("sbuf", [128, 4], "float32"), "ps": ("psum", [128, 4096], "float32"),
+}
+for _t in range(R):
+    SCRATCH["meta%d" % _t] = ("sbuf", [128, 16], "bfloat16")
+    SCRATCH["lm%d" % _t] = ("sbuf", [128, 12], "bfloat16")
+    SCRATCH["snd%d" % _t] = ("sbuf", [128, 192], CODE)
+    SCRATCH["sns%d" % _t] = ("sbuf", [128, 192], "uint8")
+    SCRATCH["land%d" % _t] = ("sbuf", [128, 768], CODE)
+    SCRATCH["lans%d" % _t] = ("sbuf", [128, 768], "uint8")
+    SCRATCH["yo%d" % _t] = ("sbuf", [128, 64], "float32")
+    SCRATCH["ido%d" % _t] = ("sbuf", [128, 4], "float32")
+for _t in range(R + 1):
+    SCRATCH["ca%d" % _t] = ("sbuf", [128, 256], CODE)
+    SCRATCH["cas%d" % _t] = ("sbuf", [128, 256], "uint8")
+SEMAPHORES = ["qv", "qs", "qt", "qp", "ldcb", "ldx0", "ldx1", "ldx2", "ldw", "st", "sent",
+              "arc0", "arc1", "arc2", "arm0", "arm1", "arm2", "ark0", "ark1", "ark2"]
+
+
+def rank_program(g, core, T, topo):
+    rank = T.rank_of(core)
+    if rank is None:
+        return
+    cores = list(T.cores)
+
+    def others(r):
+        def hops(d):
+            a, b = topo.chip(cores[r]), topo.chip(cores[d])
+            return 0 if a == b else (1 if topo.mates(a, b) or topo.same_plane(a, b) else 2)
+        return sorted([d for d in range(N) if d != r], key=lambda d: -hops(d))
+
+    def bits(es):
+        m = 0
+        for e in es:
+            m |= 1 << e
+        return m
+
+    def common(r):
+        es = topo.engines(cores[r], cores[others(r)[0]])
+        for d in others(r):
+            es = [e for e in es if e in topo.engines(cores[r], cores[d])]
+        return es
+
+    def split(r, kind):
+        es = common(r)
+        h, q = len(es) // 2, len(es) // 4
+        a, b, c = others(r)
+        if kind == 0:
+            return {a: es[:h], b: es[h:h + q], c: es[h + q:]}
+        return {a: es[h:], b: es[:q], c: es[q:h]}
+
+    oth = others(rank)
+    full = common(rank)
+    dst = {}
+    for d in oth:
+        rid, pid, _ = topo.addr(cores[d])
+        dst[d] = (rid, pid)
+    n_meta = sum(len(split(s, 0)[rank]) for s in range(N) if s != rank)
+    n_tok = sum(len(split(s, 1)[rank]) + len(common(s)) for s in range(N) if s != rank)
+    n_cen = sum(2 * len(common(s)) for s in range(N) if s != rank)
+
+    ENG = {"v": g.vector, "s": g.scalar, "t": g.tensor, "p": g, "y": g.sync}
+    cnt = {}
+    know = {q: {} for q in ENG}
+    writers, readers = {}, {}
+
+    def await_(q, recs):
+        recs = [r for r in recs if know[q].get(r[0], 0) < r[1]]
+        keep = []
+        for i, r in enumerate(recs):
+            if any(o is not r and o[2].get(r[0], 0) >= r[1] and not (o[0] == r[0] and o[1] == r[1] and j > i)
+                   for j, o in enumerate(recs)):
+                continue
+            keep.append(r)
+        for r in keep:
+            if know[q].get(r[0], 0) < r[1]:
+                ENG[q].wait_ge(T.sem[r[0]], r[1])
+            for k, v in r[2].items():
+                know[q][k] = max(know[q].get(k, 0), v)
+        for r in recs:
+            for k, v in r[2].items():
+                know[q][k] = max(know[q].get(k, 0), v)
+
+    def deps(q, rd, wr):
+        recs = []
+        for k in rd:
+            recs += [r for r in writers.get(k, [])]
+            if k[:2] == "ps":
+                recs += [r for r in readers.get(k, []) if r[3] != q]
+        for k in wr:
+            recs += writers.get(k, []) + readers.get(k, [])
+        return recs
+
+    def note(rec, rd, wr):
+        for k in wr:
+            writers[k], readers[k] = [rec], []
+        for k in rd:
+            if k not in wr:
+                readers.setdefault(k, []).append(rec)
+
+    def record(q, sem, n):
+        cnt[sem] = cnt.get(sem, 0) + n
+        clk = dict(know[q])
+        clk[sem] = cnt[sem]
+        return (sem, cnt[sem], clk, q)
+
+    def run(q, f, rd, wr):
+        await_(q, deps(q, rd, wr))
+        f(ENG[q]).then_inc(T.sem["q" + q], 1)
+        note(record(q, "q" + q, 1), rd, wr)
+
+    def dma(q, out, in_, rd, wr, sem):
+        await_(q, deps(q, rd, wr))
+        ENG[q].dma_start(out, in_).then_inc(T.sem[sem], 16)
+        note(record(q, sem, 16), rd, wr)
+
+    def arrive(sem, n, keys):
+        cnt[sem] = n
+        rec = (sem, n, {sem: n}, "r")
+        for k in keys:
+            writers.setdefault(k, []).append(rec)
+
+    def remote(transfers, rd):
+        await_("p", deps("p", rd, []))
+        g.remote_dma_fused([t for t, _ in transfers], local_sem=T.sem["sent"])
+        cnt["sent"] = cnt.get("sent", 0) + sum(n for _, n in transfers)
+
+    def one(d, src, to, sem, es):
+        return (RemoteDMATransfer(dst_ids=[DstId(rid=dst[d][0], pnc=dst[d][1])], dma_engine_mask=bits(es),
+                                  remote_sem=T.sem[sem], src=src, dst=to), len(es))
+
+    def many(src, to, sem):
+        return (RemoteDMATransfer(dst_ids=[DstId(rid=dst[d][0], pnc=dst[d][1]) for d in oth], dma_engine_mask=bits(full),
+                                  remote_sem=T.sem[sem], srcs=[src], dsts=[to for d in oth]), len(full))
+
+    def ts(out, in0, s1, s2, o0, o1, rd, wr):
+        if o1 is None:
+            run("v", lambda e: e.tensor_scalar(out, in0, s1, None, o0), rd, wr)
+        else:
+            run("v", lambda e: e.tensor_scalar(out, in0, s1, s2, o0, o1), rd, wr)
+
+    def tt(out, a, b, op, rd, wr):
+        run("v", lambda e: e.tensor_tensor(out, a, b, op), rd, wr)
+
+    def fill(ap, c, key):
+        run("v", lambda e: e.memset(ap, c), [], [key])
+
+    def cp(q, out, in_, rd, wr):
+        if q == "v":
+            run("v", lambda e: e.tensor_copy(out, in_), rd, wr)
+        else:
+            run("s", lambda e: e.activation(out, in_, AF.Copy), rd, wr)
+
+    def quant(c, s, a, b, tile, x, keys, out):
+        run("v", lambda e: e.quantize_mx(T[c][:, a:b], T[s][:, a:b], T[tile][:, x:x + 4 * (b - a)]), keys, out)
+
+    def mm(bank, n, l, la, r, ra, rd):
+        lc, lsc = l
+        rc, rs = r
+        run("t", lambda e: e.matmul_mx(T.ps[:, 512 * bank:512 * bank + n], T[lc][:, la:la + 128], T[lsc][:, la:la + 128],
+                                       T[rc][:, ra:ra + n], T[rs][:, ra:ra + n], True, True), rd, ["ps%d" % bank])
+
+    def pick(kind, dstb, da, n, srcb, sa, sb, lstb, la, rd, wr):
+        k = n // 16
+        if kind == "c":
+            run("v", lambda e: e.tensor_copy(T[dstb][:, da:da + n].bitcast(dt.uint32),
+                                             T[srcb][:, sa:sb].bitcast(dt.uint32).indirect(T[lstb][:, la:la + k])), rd, wr)
+        else:
+            run("s", lambda e: e.activation(T[dstb][:, da:da + n],
+                                            T[srcb][:, sa:sb].indirect(T[lstb][:, la:la + k]), AF.Copy), rd, wr)
+
+    def iota(out, pattern, base, mult, key, imprecise=True):
+        if imprecise:
+            run("p", lambda e: e.iota(out, pattern, base, mult, allow_small_or_imprecise_dtypes=True), [], [key])
+        else:
+            run("p", lambda e: e.iota(out, pattern, base, mult), [], [key])
+
+    def ps(bank, a, b, p0=0):
+        return T.ps[p0:128, 512 * bank + a:512 * bank + b]
+
+    dma("y", T.cbt[:, 0:128], T.cb[:, :], [], ["cbt"], "ldcb")
+    dma("s", T.xt[:, 0:768], T.x[:, 0:768], [], ["xt0"], "ldx0")
+    dma("y", T.xt[:, 768:1536], T.x[:, 768:1536], [], ["xt1"], "ldx1")
+    dma("y", T.wt[:, :], T.w[:, :], [], ["wt"], "ldw")
+    dma("y", T.xt[:, 1536:2304], T.x[:, 1536:2304], [], ["xt2"], "ldx2")
+
+    iota(T.pi[:, :], [[1, 1]], 0, 1, "pi", False)
+    iota(T.pcol[:, :], [[1, 1]], 0, 1, "pcol")
+    iota(T.rowi[:, :], [[1, 128]], 0, 0, "rowi")
+    iota(T.k16[:, :], [[0, 8], [1, 16]], 0, 0, "k16")
+
+    fill(T.cbt[:, 128:512], 0.0, "cbtz")
+    ts(T.qi[:, :], T.pi[:, :], 15, None, A.bitwise_and, None, ["pi"], ["qi"])
+    cp("v", T.qcol[:, :], T.qi[:, :], ["qi"], ["qcol"])
+    for h in range(2):
+        ts(T.ilst[:, h:h + 1], T.qcol[:, :], 16.0 * h, None, A.add, None, ["qcol"], ["ilst%d" % h])
+    fill(T.negc[:, :], LOW, "negc")
+    fill(T.pt[:, :], 0.0, "pt")
+
+    quant("cbq", "cbs", 0, 128, "cbt", 0, ["cbt", "cbtz"], ["cbq"])
+    own = slice(G * rank, G * rank + G)
+    remote([many(T.cbq[:, 0:G].bitcast(dt.uint8), T.ca0[:, own].bitcast(dt.uint8), "arc0")], ["cbq"])
+    remote([many(T.cbs[:, 0:G], T.cas0[:, own], "arc0")], ["cbq"])
+    pick("c", "ca0", G * rank, G, "cbq", 0, 128, "ilst", 0, ["cbq", "ilst0", "ilst1"], ["ca0"])
+    pick("s", "cas0", G * rank, G, "cbs", 0, 128, "ilst", 0, ["cbq", "ilst0", "ilst1"], ["cas0"])
+    arrive("arc0", n_cen, ["ca0", "cas0"])
+    quant("xq", "xs", 0, 192, "xt", 0, ["xt0"], ["xq0"])
+    order = [rank] + [s for s in range(N) if s != rank]
+    for h in range(2):
+        for e, s in enumerate(order):
+            iota(T.offi[:, 16 * h + 4 * e:16 * h + 4 * e + 4], [[16, 4]], 64 * s, 0, "offi%d%d" % (h, e))
+        iota(T.pen[:, 16 * h:16 * h + 16], [[0, 4], [1 - 2 * h, 2], [0, 2]], h, 0, "pen%d" % h)
+    offk = ["offi%d%d" % (h, e) for h in range(2) for e in range(4)]
+
+    fill(T.pt[:, 0:1], 1.0, "pt")
+    fill(T.pt[64:128, 1:2], 1.0, "pt")
+    fill(T.pt[:, 512:513], 1.0, "pt")
+    fill(T.pt[64:128, 513:514], 1.0, "pt")
+    fill(T.pt[0:64, 513:528:4], 1.0, "pt")
+    for c0 in (0, 512):
+        k = "ct%d" % c0
+        if c0 == 0:
+            ts(T.ct[:, 0:512:4], T.rowi[:, :], T.pcol[:, :], None, A.is_ge, None, ["rowi", "pcol"], [k + "a"])
+            ts(T.ct[:, 2:512:4], T.rowi[:, :], T.pcol[:, :], -1.0, A.is_ge, A.mult, ["rowi", "pcol"], [k + "b"])
+            fill(T.ct[64:128, 1:512:4], 0.0, k + "c")
+            fill(T.ct[:, 3:512:4], 0.0, k + "d")
+        else:
+            fill(T.ct[:, 512:1024:4], 1.0, k + "a")
+            fill(T.ct[:, 514:1024:4], -1.0, k + "b")
+            ts(T.ct[64:128, 513:1024:4], T.rowi[64:128, :], T.pcol[64:128, :], None, A.is_ge, None, ["rowi", "pcol"], [k + "c"])
+            ts(T.ct[64:128, 515:1024:4], T.rowi[64:128, :], T.pcol[64:128, :], -1.0, A.is_ge, A.mult, ["rowi", "pcol"], [k + "d"])
+            fill(T.ct[0:64, 515:1024:4], 0.0, k + "f")
+        fill(T.ct[0:64, c0 + 1:c0 + 512:4], -1.0, k + "e")
+    for t in range(4):
+        fill(T.ct[:, 1024 + t:1536:4], 1.0 if t < 2 else 0.0, "ct1024%d" % t)
+        fill(T.ct[:, 1536 + t:2048:4], -1.0 if t < 2 else 1.0, "ct1536%d" % t)
+    quant("cq", "cqs", 0, 512, "ct", 0, ["ct0a", "ct0b", "ct0c", "ct0d", "ct0e", "ct512a", "ct512b", "ct512c", "ct512d",
+                                         "ct512e", "ct512f"] + ["ct1024%d" % t for t in range(4)]
+          + ["ct1536%d" % t for t in range(4)], ["cq"])
+    fill(T.zz[:, :], 0.0, "zz")
+    ts(T.qcol1[:, :], T.qcol[:, :], 1.0, None, A.add, None, ["qcol"], ["qcol1"])
+    ts(T.corr[:, :], T.qcol[:, :], 15.0, 1024.0, A.is_lt, A.mult, ["qcol"], ["corr"])
+    ts(T.ncorr[:, :], T.corr[:, :], -1.0, None, A.mult, None, ["corr"], ["ncorr"])
+    ts(T.msk[:, :], T.k16[:, :], T.qcol[:, :], -4096.0, A.is_equal, A.mult, ["k16", "qcol"], ["msk"])
+    ts(T.msk2[:, :], T.k16[:, :], T.qcol1[:, :], 1024.0, A.is_equal, A.mult, ["k16", "qcol1"], ["msk2"])
+    tt(T.msk[:, :], T.msk[:, :], T.msk2[:, :], A.add, ["msk2"], ["msk"])
+
+    def late_constants():
+        ts(T.cv[:, :], T.offi[:, :], T.qcol[:, :], 512.0, A.add, A.mult, offk + ["qcol"], ["cv"])
+        ts(T.pen[:, :], T.pen[:, :], PEN, None, A.mult, None, [], ["pen0", "pen1"])
+        tt(T.cv[:, :], T.cv[:, :], T.pen[:, :], A.add, ["pen0", "pen1"], ["cv"])
+        fill(T.rsa[:, :], -FAR, "rsa")
+        fill(T.rsb[:, :], -FAR, "rsb")
+        fill(T.rsa[:, 16:17], FAR, "rsa")
+        fill(T.rsb[:, 17:18], FAR, "rsb")
+        for h in range(2):
+            ts(T.gnew[:, h:h + 1], T.qcol[:, :], 128.0 + 16 * h, None, A.add, None, ["qcol"], ["gnew%d" % h])
+        fill(T.zt[:, :], 0.0, "zt")
+        quant("land0", "lans0", 512, 768, "zt", 0, ["zt"], ["lz0"])
+        quant("adm", "adms", 0, 128, "zt", 0, ["zt"], ["adm", "adms"])
+        fill(T.nt[:, :], 0.0, "nt")
+        fill(T.et[:, :], 0.0, "et")
+        for b in range(4):
+            ts(T.et[:, 512 * b + b:512 * b + 512:4], T.rowi[:, :], T.pcol[:, :], 0.25, A.is_equal, A.mult,
+               ["rowi", "pcol"], ["et"])
+        quant("eq", "eqs", 0, 512, "et", 0, ["et"], ["eq"])
+
+    XQ, CQ, EQ = ("xq", "xs"), ("cq", "cqs"), ("eq", "eqs")
+    for t in range(R):
+        ca, cas = "ca%d" % t, "cas%d" % t
+        CA = (ca, cas)
+        lm, meta = T["lm%d" % t], T["meta%d" % t]
+        land, lans, snd, sns = "land%d" % t, "lans%d" % t, "snd%d" % t, "sns%d" % t
+        mm(0, 128, XQ, 192 * t, CA, 0, ["xq%d" % t, ca, cas])
+        mm(1, 128, XQ, 192 * t + 64, CA, 0, ["xq%d" % t, ca, cas])
+        for bank, m, p0 in ((0, T.ma, 0), (1, T.mb, 64)):
+            key = "ma" if bank == 0 else "mb"
+            run("v", lambda e: e.tensor_tensor_scan(m[p0:128, :], ps(bank, 0, 128, p0), T.negc[p0:128, :], LOW, A.max, A.max),
+                ["ps%d" % bank, "negc"], [key])
+
+        def before(q, m, key, p0, el, k0, k1, step, oc, wr):
+            n = len(range(k0, k1, step))
+            out = T.pt[p0:128, 4 * oc + el:min(4 * (oc + n), 528):4]
+            if q == "v":
+                ts(out, m[p0:128, k0:k1:step], m[p0:128, 127:128], None, A.is_lt, None, [key], [wr])
+            else:
+                run("s", lambda e: e.activation(out, m[p0:128, k0:k1:step], AF.Sign, bias=m[p0:128, 127:128], scale=-1.0),
+                    [key], [wr])
+        if t == 0:
+            await_("s", writers["pt"] + writers["zz"])
+            await_("v", writers["pt"] + writers["zz"])
+        before("s", T.ma, "ma", 0, 0, 0, 127, 1, 1, "pt0")
+        before("s", T.ma, "ma", 0, 2, 0, 128, 1, 0, "pt2")
+        before("s", T.ma, "ma", 0, 0, 31, 96, 32, 129, "pt0x")
+        before("s", T.ma, "ma", 0, 2, 31, 128, 32, 128, "pt2x")
+        before("v", T.mb, "mb", 64, 1, 0, 127, 1, 1, "pt1")
+        before("v", T.mb, "mb", 64, 3, 0, 128, 1, 0, "pt3")
+        before("s", T.mb, "mb", 64, 1, 31, 96, 32, 129, "pt1x")
+        before("v", T.mb, "mb", 64, 3, 31, 128, 32, 128, "pt3x")
+        quant("pq", "pqs", 0, 132, "pt", 0, ["pt", "pt0", "pt1", "pt2", "pt3", "pt0x", "pt1x", "pt2x", "pt3x"], ["pq"])
+        mm(2, 132, CQ, 0, ("pq", "pqs"), 0, ["cq", "pq"])
+        mm(3, 132, CQ, 128, ("pq", "pqs"), 0, ["cq", "pq"])
+
+        def below1(bank, p0, el, wr):
+            ts(T.zz[p0:128, el:528:4], ps(bank, 0, 132, p0), 1.0, None, A.is_lt, None, ["ps%d" % bank], [wr])
+
+        def below2(bank, p0, el, wr):
+            run("s", lambda e: e.activation(T.zz[p0:128, el:512:4], ps(bank, 0, 128, p0), AF.Relu, bias=2.0, scale=-1.0),
+                ["ps%d" % bank], [wr])
+        below1(2, 0, 0, "zz0")
+        below2(3, 64, 3, "zz3")
+        below1(3, 64, 1, "zz1")
+        below2(2, 0, 2, "zz2")
+        quant("zq", "zqs", 0, 132, "zz", 0, ["zz", "zz0", "zz1", "zz2", "zz3"], ["zq"])
+        mm(4, 132, CQ, 256, ("zq", "zqs"), 0, ["cq", "zq"])
+        mm(5, 132, CQ, 384, ("zq", "zqs"), 0, ["cq", "zq"])
+        for j, ls in ((0, T.ls1), (1, T.ls2)):
+            run("v", lambda e: e.tensor_tensor_scan(ls[:, :], T.msk[:, :], ps(4 + j, 0, 128), 0.0, A.add, A.max),
+                ["ps%d" % (4 + j), "msk"], ["ls%d" % j])
+        for j, ls in ((0, T.ls1), (1, T.ls2)):
+            run("s", lambda e: e.activation(T.ii[:, j:16:2], ls[:, 15:128:16], AF.Identity, bias=T.ncorr[:, 0:1], scale=1.0),
+                ["ls%d" % j, "ncorr"], ["ii%d" % j])
+            ts(T.lst[:, j:16:2], ls[:, 15:128:16], T.corr[:, 0:1], float(TOK - 1), A.subtract, A.min,
+               ["ls%d" % j, "corr"], ["lst%d" % j])
+        LST = ["lst0", "lst1"]
+        mk = "meta%d" % t
+        sp0, sp1 = split(rank, 0), split(rank, 1)
+        me = slice(64 * rank, 64 * rank + 64)
+
+        def slots(kind, n):
+            d = (oth + [rank])[n]
+            b, x = (snd, "xq") if kind == "c" else (sns, "xs")
+            o = land if kind == "c" else lans
+            if n < 3:
+                pick(kind, b, 64 * n, 64, x, 192 * t, 192 * t + 192, "lst", 4 * d, LST + ["xq%d" % t], ["%s.%d" % (b, n)])
+            else:
+                pick(kind, o, 64 * rank, 64, x, 192 * t, 192 * t + 192, "lst", 4 * d, LST + ["xq%d" % t], [o])
+
+        def send_codes(n):
+            remote([one(oth[n], T[snd][:, 64 * n:64 * n + 64].bitcast(dt.uint8), T[land][:, me].bitcast(dt.uint8), "ark%d" % t, full)],
+                   ["%s.%d" % (snd, n)])
+
+        def place(d):
+            e = [s for s in range(N) if s != d].index(rank)
+            return slice(4 * e, 4 * e + 4)
+        for n in range(4):
+            slots("s", n)
+        slots("c", 0)
+        send_codes(0)
+        for d in range(N):
+            ts(T.tt[:, 4 * d:4 * d + 4], T.ii[:, 4 * d:4 * d + 4], ps(4, 128 + d, 129 + d), BIG, A.is_ge, A.mult,
+               ["ii0", "ii1", "ps4"], ["tt%d" % d])
+        tt(meta[:, :], T.ii[:, :], T.tt[:, :], A.add, ["ii0", "ii1", "tt0", "tt1", "tt2", "tt3"], [mk])
+        remote([one(d, meta[:, 4 * d:4 * d + 4], lm[:, place(d)], "arm%d" % t, sp0[d]) for d in oth], [mk])
+        slots("c", 1)
+        send_codes(1)
+        remote([one(e, T[sns][:, 64 * m:64 * m + 64], T[lans][:, me], "ark%d" % t, sp1[e]) for m, e in enumerate(oth)],
+               ["%s.%d" % (sns, m) for m in range(3)])
+        slots("c", 2)
+        send_codes(2)
+        slots("c", 3)
+        if t == 0:
+            late_constants()
+        for h in range(2):
+            tt(T.vv[:, 16 * h:16 * h + 4], meta[:, 4 * rank:4 * rank + 4], T.cv[:, 16 * h:16 * h + 4], A.add,
+               [mk, "cv"], ["vvo%d" % h])
+        for b in range(4):
+            mm(4 + b, 128, EQ, 128 * b, CA, 0, ["eq", ca, cas])
+        for b in range(4):
+            run("s", lambda e: e.activation(T.hc[:, 32 * b:32 * b + 32], ps(4 + b, G * rank, G * rank + G), AF.Copy, scale=2.0),
+                ["ps%d" % (4 + b)], ["hc%d" % b])
+        if t == 0:
+            quant("xq", "xs", 192, 384, "xt", 768, ["xt1"], ["xq1"])
+            quant("wq", "ws", 0, 128, "wt", 0, ["wt"], ["wq"])
+        if t == 1:
+            quant("xq", "xs", 384, 576, "xt", 1536, ["xt2"], ["xq2"])
+        if t < 2:
+            quant("land%d" % (t + 1), "lans%d" % (t + 1), 512, 768, "zt", 0, ["zt"], ["lz%d" % (t + 1)])
+        arrive("arm%d" % t, n_meta, ["lm%d" % t])
+        for h in range(2):
+            tt(T.vv[:, 16 * h + 4:16 * h + 16], lm[:, :], T.cv[:, 16 * h + 4:16 * h + 16], A.add, ["lm%d" % t, "cv"], ["vvr%d" % h])
+        VV = ["vvo0", "vvo1", "vvr0", "vvr1"]
+        run("v", lambda e: e.tensor_tensor_scan(T.pm[:, :], T.rsa[:, :], T.vv[:, :], FAR, A.max, A.min), VV + ["rsa"], ["pm"])
+        tt(T.mx[:, 1:32], T.vv[:, 1:32], T.pm[:, 0:31], A.max, VV + ["pm"], ["mx"])
+        ts(T.alst[:, 0:2], T.pm[:, 15:32:16], 1.0 / 512, None, A.mult, None, ["pm"], ["alst0"])
+        run("v", lambda e: e.tensor_tensor_scan(T.sc[:, 1:32], T.rsb[:, 1:32], T.mx[:, 1:32], FAR, A.max, A.min),
+            ["mx", "rsb"], ["sc"])
+        for h in range(2):
+            c = T.sc[:, 15 + 16 * h:16 + 16 * h]
+            ts(T.sz[:, h:h + 1], c, BIG, c, A.is_lt, A.mult, ["sc"], ["sz%d" % h])
+        ts(T.alst[:, 2:4], T.sc[:, 15:32:16], 1.0 / 512, None, A.mult, None, ["sc"], ["alst1"])
+        for h in range(2):
+            ts(T.alst[:, 4 + h:5 + h], T.sz[:, h:h + 1], T.pm[:, 15 + 16 * h:16 + 16 * h], 1.0 / 512, A.max, A.mult,
+               ["sz%d" % h, "pm"], ["alst%d" % (2 + h)])
+        arrive("ark%d" % t, n_tok, [land, lans])
+        AL = ["alst0", "alst1", "alst2", "alst3", "lz%d" % t]
+        pick("c", "adm", 0, 96, land, 0, 768, "alst", 0, AL + [land], ["adm"])
+        pick("s", "adms", 0, 96, lans, 0, 768, "alst", 0, AL + [lans], ["adms"])
+        for b in range(4):
+            mm(b, 128, EQ, 128 * b, ("adm", "adms"), 0, ["eq", "adm", "adms"])
+        mm(6, 128, ("wq", "ws"), 0, ("adm", "adms"), 0, ["wq", "adm", "adms"])
+        ts(T.mv[:, :], T.pm[:, 15:32:16], BIG, float(G * rank - 128), A.is_ge, A.mult, ["pm"], ["mv"])
+        for h in range(2):
+            ts(T.clst[:, h:h + 1], T.mv[:, h:h + 1], T.gnew[:, h:h + 1], None, A.add, None, ["mv", "gnew%d" % h], ["clst%d" % h])
+        if t == 0:
+            await_("v", writers["nt"])
+        for b in range(4):
+            run("s", lambda e: e.activation(T.s4[:, 32 * b:32 * b + 32], ps(b, 64, 96), AF.Copy), ["ps%d" % b], ["s4%d" % b])
+        for b in range(5):
+            if b < 4:
+                tt(T.hh[:, 32 * b:32 * b + 32], ps(b, 0, 32), T.s4[:, 32 * b:32 * b + 32], A.add, ["ps%d" % b, "s4%d" % b], ["hh%d" % b])
+            if b > 0:
+                a = b - 1
+                tt(T.nt[:, a:128:4], T.hh[:, 32 * a:32 * a + 32], T.hc[:, 32 * a:32 * a + 32], A.add, ["hh%d" % a, "hc%d" % a], ["nt%d" % a])
+        run("v", lambda e: e.quantize_mx(T[ca][:, 128:256], T[cas][:, 128:256], T.nt[:, :]), ["nt", "nt0", "nt1", "nt2", "nt3"], [ca + "n"])
+        cn, cns = "ca%d" % (t + 1), "cas%d" % (t + 1)
+        CL = ["clst0", "clst1", ca + "n"]
+        pick("c", cn, G * rank, G, ca, 0, 256, "clst", 0, CL + [ca], [cn])
+        pick("s", cns, G * rank, G, cas, 0, 256, "clst", 0, CL + [cas], [cns])
+        if t < R - 1:
+            remote([many(T[cn][:, own].bitcast(dt.uint8), T[cn][:, own].bitcast(dt.uint8), "arc%d" % (t + 1))], [cn])
+            remote([many(T[cns][:, own], T[cns][:, own], "arc%d" % (t + 1))], [cns])
+        else:
+            dma("y", T.oc[:, :], T[cn][:, own].bitcast(dt.uint8), [cn], [], "st")
+            for k in range(4):
+                dma("y" if k % 2 else "s", T.osc[4 * k:4 * k + 4, :], T[cns][32 * k:32 * k + 4, own], [cns], [], "st")
+        yo, ido = T["yo%d" % t], T["ido%d" % t]
+        for i in range(2):
+            run("s", lambda e: e.activation(yo[:, i:64:2], ps(6, 32 * i, 32 * i + 32), AF.Copy), ["ps6"], ["yo%d%d" % (t, i)])
+        dma("y", T.y[:, 64 * t:64 * t + 64], yo[:, :], ["yo%d0" % t, "yo%d1" % t], [], "st")
+        cp("v", T.vi[:, 0:4:2], T.pm[:, 15:32:16], ["pm"], ["vi0"])
+        cp("v", T.vi[:, 1:4:2], T.sc[:, 15:32:16], ["sc"], ["vi1"])
+        VI = ["vi0", "vi1"]
+        ts(T.sv[:, :], T.vi[:, :], 15, None, A.arith_shift_right, None, VI, ["sv"])
+        ts(T.iv[:, :], T.vi[:, :], 511, None, A.bitwise_and, None, VI, ["iv"])
+        ts(T.val[:, :], T.vi[:, :], BIG, None, A.is_lt, None, VI, ["val"])
+        ts(T.s192[:, :], T.sv[:, :], float(TOK), 1.0, A.mult, A.add, ["sv"], ["s192"])
+        tt(T.idf[:, :], T.s192[:, :], T.iv[:, :], A.add, ["s192", "iv"], ["idf"])
+        tt(T.idg[:, :], T.idf[:, :], T.val[:, :], A.mult, ["idf", "val"], ["idg"])
+        ts(ido[:, :], T.idg[:, :], -1.0, None, A.add, None, ["idg"], ["ido%d" % t])
+        for h in range(2):
+            dma("y", T.ids[0:1, 64 * t + 32 * h:64 * t + 32 * h + 32], ido[0:16, 2 * h:2 * h + 2], ["ido%d" % t], [], "st")
+        if t < R - 1:
+            arrive("arc%d" % (t + 1), n_cen, [cn, cns])
+    for k in cnt:
+        if know["p"].get(k, 0) < cnt[k]:
+            g.wait_ge(T.sem[k], cnt[k])

@@ -12,31 +12,24 @@ SCRATCH = {
     "cbt": ("sbuf", [128, 512], "bfloat16"), "xt": ("sbuf", [128, 2304], "bfloat16"), "wt": ("sbuf", [128, 512], "bfloat16"),
     "zt": ("sbuf", [128, 1024], "bfloat16"), "pt": ("sbuf", [128, 528], "bfloat16"), "zz": ("sbuf", [128, 528], "bfloat16"),
     "nt": ("sbuf", [128, 512], "bfloat16"), "ct": ("sbuf", [128, 2048], "bfloat16"), "et": ("sbuf", [128, 2048], "bfloat16"),
-    "cq": ("sbuf", [128, 512], CODE), "cqs": ("sbuf", [128, 512], "uint8"),
-    "eq": ("sbuf", [128, 512], CODE), "eqs": ("sbuf", [128, 512], "uint8"),
-    "cbq": ("sbuf", [128, 128], CODE), "cbs": ("sbuf", [128, 128], "uint8"),
-    "xq": ("sbuf", [128, 576], CODE), "xs": ("sbuf", [128, 576], "uint8"),
-    "wq": ("sbuf", [128, 128], CODE), "ws": ("sbuf", [128, 128], "uint8"),
-    "pq": ("sbuf", [128, 132], CODE), "pqs": ("sbuf", [128, 132], "uint8"),
-    "zq": ("sbuf", [128, 132], CODE), "zqs": ("sbuf", [128, 132], "uint8"),
-    "adm": ("sbuf", [128, 128], CODE), "adms": ("sbuf", [128, 128], "uint8"),
-    "rowi": ("sbuf", [128, 128], "float32"), "k16": ("sbuf", [128, 128], "float32"), "negc": ("sbuf", [128, 128], "float32"),
-    "ma": ("sbuf", [128, 128], "float32"), "mb": ("sbuf", [128, 128], "float32"), "msk": ("sbuf", [128, 128], "float32"),
-    "msk2": ("sbuf", [128, 128], "float32"), "ls1": ("sbuf", [128, 128], "float32"), "ls2": ("sbuf", [128, 128], "float32"),
-    "pcol": ("sbuf", [128, 1], "float32"), "pi": ("sbuf", [128, 1], "int32"), "qi": ("sbuf", [128, 1], "int32"),
-    "qcol": ("sbuf", [128, 1], "float32"), "qcol1": ("sbuf", [128, 1], "float32"), "corr": ("sbuf", [128, 1], "float32"),
-    "ncorr": ("sbuf", [128, 1], "float32"),
-    "ii": ("sbuf", [128, 16], "float32"), "tt": ("sbuf", [128, 16], "float32"), "lst": ("sbuf", [128, 16], "uint16"),
-    "offi": ("sbuf", [128, 32], "float32"), "pen": ("sbuf", [128, 32], "float32"), "cv": ("sbuf", [128, 32], "float32"),
-    "vv": ("sbuf", [128, 32], "float32"), "pm": ("sbuf", [128, 32], "float32"), "mx": ("sbuf", [128, 32], "float32"),
-    "sc": ("sbuf", [128, 32], "float32"), "rsa": ("sbuf", [128, 32], "float32"), "rsb": ("sbuf", [128, 32], "float32"),
-    "sz": ("sbuf", [128, 2], "float32"), "alst": ("sbuf", [128, 6], "uint16"), "mv": ("sbuf", [128, 2], "float32"),
-    "clst": ("sbuf", [128, 2], "uint16"), "ilst": ("sbuf", [128, 2], "uint16"), "gnew": ("sbuf", [128, 2], "float32"),
-    "s4": ("sbuf", [128, 128], "float32"), "hh": ("sbuf", [128, 128], "float32"), "hc": ("sbuf", [128, 128], "float32"),
-    "vi": ("sbuf", [128, 4], "int32"), "iv": ("sbuf", [128, 4], "int32"), "sv": ("sbuf", [128, 4], "int32"),
-    "s192": ("sbuf", [128, 4], "float32"), "idf": ("sbuf", [128, 4], "float32"), "val": ("sbuf", [128, 4], "float32"),
     "idg": ("sbuf", [128, 4], "float32"), "ps": ("psum", [128, 4096], "float32"),
 }
+for _c, _s, _n in (("cq", "cqs", 512), ("eq", "eqs", 512), ("cbq", "cbs", 128), ("xq", "xs", 576), ("wq", "ws", 128),
+                   ("pq", "pqs", 132), ("zq", "zqs", 132), ("adm", "adms", 128)):
+    SCRATCH[_c] = ("sbuf", [128, _n], CODE)
+    SCRATCH[_s] = ("sbuf", [128, _n], "uint8")
+for _b in ("rowi", "k16", "negc", "ma", "mb", "msk", "msk2", "ls1", "ls2", "s4", "hh", "hc"):
+    SCRATCH[_b] = ("sbuf", [128, 128], "float32")
+for _b in ("pcol", "qcol", "qcol1", "corr", "ncorr"):
+    SCRATCH[_b] = ("sbuf", [128, 1], "float32")
+for _b in ("offi", "pen", "cv", "vv", "mx", "rsa", "rsb"):
+    SCRATCH[_b] = ("sbuf", [128, 32], "float32")
+SCRATCH["pmsc"] = ("sbuf", [128, 64], "float32")
+for _b, _n, _d in (("pi", 1, "int32"), ("qi", 1, "int32"), ("ii", 16, "float32"), ("tt", 16, "float32"), ("lst", 16, "uint16"),
+                   ("sz", 2, "float32"), ("alst", 6, "uint16"), ("mv", 2, "float32"), ("clst", 2, "uint16"),
+                   ("ilst", 2, "uint16"), ("gnew", 2, "float32"), ("vi", 4, "int32"), ("iv", 4, "int32"), ("sv", 4, "int32"),
+                   ("s192", 4, "float32"), ("idf", 4, "float32"), ("val", 4, "float32")):
+    SCRATCH[_b] = ("sbuf", [128, _n], _d)
 for _t in range(R):
     SCRATCH["meta%d" % _t] = ("sbuf", [128, 16], "bfloat16")
     SCRATCH["lm%d" % _t] = ("sbuf", [128, 12], "bfloat16")
@@ -181,11 +174,8 @@ def rank_program(g, core, T, topo):
     def fill(ap, c, key):
         run("v", lambda e: e.memset(ap, c), [], [key])
 
-    def cp(q, out, in_, rd, wr):
-        if q == "v":
-            run("v", lambda e: e.tensor_copy(out, in_), rd, wr)
-        else:
-            run("s", lambda e: e.activation(out, in_, AF.Copy), rd, wr)
+    def flat(out, in_, c, rd, key):
+        run("s", lambda e: e.activation(out, in_, AF.Identity, bias=c, scale=0.0), rd, [key])
 
     def quant(c, s, a, b, tile, x, keys, out):
         run("v", lambda e: e.quantize_mx(T[c][:, a:b], T[s][:, a:b], T[tile][:, x:x + 4 * (b - a)]), keys, out)
@@ -221,17 +211,25 @@ def rank_program(g, core, T, topo):
     dma("y", T.xt[:, 1536:2304], T.x[:, 1536:2304], [], ["xt2"], "ldx2")
 
     iota(T.pi[:, :], [[1, 1]], 0, 1, "pi", False)
-    iota(T.pcol[:, :], [[1, 1]], 0, 1, "pcol")
     iota(T.rowi[:, :], [[1, 128]], 0, 0, "rowi")
+    iota(T.pcol[:, :], [[1, 1]], 0, 1, "pcol")
     iota(T.k16[:, :], [[0, 8], [1, 16]], 0, 0, "k16")
-
+    for t in range(4):
+        flat(T.ct[:, 1024 + t:1536:4], T.rowi[:, :], 1.0 if t < 2 else 0.0, ["rowi"], "ct1024%d" % t)
+        flat(T.ct[:, 1536 + t:2048:4], T.rowi[:, :], -1.0 if t < 2 else 1.0, ["rowi"], "ct1536%d" % t)
+    flat(T.ct[:, 3:512:4], T.rowi[:, :], 0.0, ["rowi"], "ct0d")
+    flat(T.ct[:, 512:1024:4], T.rowi[:, :], 1.0, ["rowi"], "ct512a")
+    flat(T.ct[:, 514:1024:4], T.rowi[:, :], -1.0, ["rowi"], "ct512b")
     fill(T.cbt[:, 128:512], 0.0, "cbtz")
+    fill(T.pt[:, :], 0.0, "pt")
     ts(T.qi[:, :], T.pi[:, :], 15, None, A.bitwise_and, None, ["pi"], ["qi"])
-    cp("v", T.qcol[:, :], T.qi[:, :], ["qi"], ["qcol"])
+    fill(T.negc[:, :], LOW, "negc")
+    run("v", lambda e: e.tensor_copy(T.qcol[:, :], T.qi[:, :]), ["qi"], ["qcol"])
+    fill(T.ct[64:128, 1:512:4], 0.0, "ct0c")
     for h in range(2):
         ts(T.ilst[:, h:h + 1], T.qcol[:, :], 16.0 * h, None, A.add, None, ["qcol"], ["ilst%d" % h])
-    fill(T.negc[:, :], LOW, "negc")
-    fill(T.pt[:, :], 0.0, "pt")
+    ts(T.ct[:, 0:512:4], T.rowi[:, :], T.pcol[:, :], None, A.is_ge, None, ["rowi", "pcol"], ["ct0a"])
+    ts(T.ct[:, 2:512:4], T.rowi[:, :], T.pcol[:, :], -1.0, A.is_ge, A.mult, ["rowi", "pcol"], ["ct0b"])
 
     quant("cbq", "cbs", 0, 128, "cbt", 0, ["cbt", "cbtz"], ["cbq"])
     own = slice(G * rank, G * rank + G)
@@ -248,64 +246,55 @@ def rank_program(g, core, T, topo):
         iota(T.pen[:, 16 * h:16 * h + 16], [[0, 4], [1 - 2 * h, 2], [0, 2]], h, 0, "pen%d" % h)
     offk = ["offi%d%d" % (h, e) for h in range(2) for e in range(4)]
 
+    ts(T.ct[64:128, 513:1024:4], T.rowi[64:128, :], T.pcol[64:128, :], None, A.is_ge, None, ["rowi", "pcol"], ["ct512c"])
+    ts(T.ct[64:128, 515:1024:4], T.rowi[64:128, :], T.pcol[64:128, :], -1.0, A.is_ge, A.mult, ["rowi", "pcol"], ["ct512d"])
+    fill(T.ct[0:64, 1:512:4], -1.0, "ct0e")
+    fill(T.ct[0:64, 513:1024:4], -1.0, "ct512e")
+    fill(T.ct[0:64, 515:1024:4], 0.0, "ct512f")
+    quant("cq", "cqs", 0, 512, "ct", 0, ["ct0a", "ct0b", "ct0c", "ct0d", "ct0e", "ct512a", "ct512b", "ct512c", "ct512d",
+                                         "ct512e", "ct512f"] + ["ct1024%d" % t for t in range(4)]
+          + ["ct1536%d" % t for t in range(4)], ["cq"])
     fill(T.pt[:, 0:1], 1.0, "pt")
     fill(T.pt[64:128, 1:2], 1.0, "pt")
     fill(T.pt[:, 512:513], 1.0, "pt")
     fill(T.pt[64:128, 513:514], 1.0, "pt")
     fill(T.pt[0:64, 513:528:4], 1.0, "pt")
-    for c0 in (0, 512):
-        k = "ct%d" % c0
-        if c0 == 0:
-            ts(T.ct[:, 0:512:4], T.rowi[:, :], T.pcol[:, :], None, A.is_ge, None, ["rowi", "pcol"], [k + "a"])
-            ts(T.ct[:, 2:512:4], T.rowi[:, :], T.pcol[:, :], -1.0, A.is_ge, A.mult, ["rowi", "pcol"], [k + "b"])
-            fill(T.ct[64:128, 1:512:4], 0.0, k + "c")
-            fill(T.ct[:, 3:512:4], 0.0, k + "d")
-        else:
-            fill(T.ct[:, 512:1024:4], 1.0, k + "a")
-            fill(T.ct[:, 514:1024:4], -1.0, k + "b")
-            ts(T.ct[64:128, 513:1024:4], T.rowi[64:128, :], T.pcol[64:128, :], None, A.is_ge, None, ["rowi", "pcol"], [k + "c"])
-            ts(T.ct[64:128, 515:1024:4], T.rowi[64:128, :], T.pcol[64:128, :], -1.0, A.is_ge, A.mult, ["rowi", "pcol"], [k + "d"])
-            fill(T.ct[0:64, 515:1024:4], 0.0, k + "f")
-        fill(T.ct[0:64, c0 + 1:c0 + 512:4], -1.0, k + "e")
-    for t in range(4):
-        fill(T.ct[:, 1024 + t:1536:4], 1.0 if t < 2 else 0.0, "ct1024%d" % t)
-        fill(T.ct[:, 1536 + t:2048:4], -1.0 if t < 2 else 1.0, "ct1536%d" % t)
-    quant("cq", "cqs", 0, 512, "ct", 0, ["ct0a", "ct0b", "ct0c", "ct0d", "ct0e", "ct512a", "ct512b", "ct512c", "ct512d",
-                                         "ct512e", "ct512f"] + ["ct1024%d" % t for t in range(4)]
-          + ["ct1536%d" % t for t in range(4)], ["cq"])
     fill(T.zz[:, :], 0.0, "zz")
     ts(T.qcol1[:, :], T.qcol[:, :], 1.0, None, A.add, None, ["qcol"], ["qcol1"])
     ts(T.corr[:, :], T.qcol[:, :], 15.0, 1024.0, A.is_lt, A.mult, ["qcol"], ["corr"])
-    ts(T.ncorr[:, :], T.corr[:, :], -1.0, None, A.mult, None, ["corr"], ["ncorr"])
     ts(T.msk[:, :], T.k16[:, :], T.qcol[:, :], -4096.0, A.is_equal, A.mult, ["k16", "qcol"], ["msk"])
     ts(T.msk2[:, :], T.k16[:, :], T.qcol1[:, :], 1024.0, A.is_equal, A.mult, ["k16", "qcol1"], ["msk2"])
+    ts(T.ncorr[:, :], T.corr[:, :], -1.0, None, A.mult, None, ["corr"], ["ncorr"])
     tt(T.msk[:, :], T.msk[:, :], T.msk2[:, :], A.add, ["msk2"], ["msk"])
+    for b in range(4):
+        flat(T.et[:, 512 * b:512 * b + 512], T.cbt[:, :], 0.0, ["cbt", "cbtz"], "et%d" % b)
+    for b in range(4):
+        ts(T.et[:, 512 * b + b:512 * b + 512:4], T.rowi[:, :], T.pcol[:, :], 0.25, A.is_equal, A.mult,
+           ["rowi", "pcol"], ["et%d" % b])
+    quant("eq", "eqs", 0, 512, "et", 0, ["et%d" % b for b in range(4)], ["eq"])
 
     def late_constants():
+        for b in range(2):
+            flat(T.zt[:, 512 * b:512 * b + 512], T.cbt[:, :], 0.0, ["cbt", "cbtz"], "zt%d" % b)
+        flat(T.nt[:, :], T.cbt[:, :], 0.0, ["cbt", "cbtz"], "nt")
         ts(T.cv[:, :], T.offi[:, :], T.qcol[:, :], 512.0, A.add, A.mult, offk + ["qcol"], ["cv"])
         ts(T.pen[:, :], T.pen[:, :], PEN, None, A.mult, None, [], ["pen0", "pen1"])
-        tt(T.cv[:, :], T.cv[:, :], T.pen[:, :], A.add, ["pen0", "pen1"], ["cv"])
         fill(T.rsa[:, :], -FAR, "rsa")
+        tt(T.cv[:, :], T.cv[:, :], T.pen[:, :], A.add, ["pen0", "pen1"], ["cv"])
         fill(T.rsb[:, :], -FAR, "rsb")
         fill(T.rsa[:, 16:17], FAR, "rsa")
         fill(T.rsb[:, 17:18], FAR, "rsb")
         for h in range(2):
             ts(T.gnew[:, h:h + 1], T.qcol[:, :], 128.0 + 16 * h, None, A.add, None, ["qcol"], ["gnew%d" % h])
-        fill(T.zt[:, :], 0.0, "zt")
-        quant("land0", "lans0", 512, 768, "zt", 0, ["zt"], ["lz0"])
-        quant("adm", "adms", 0, 128, "zt", 0, ["zt"], ["adm", "adms"])
-        fill(T.nt[:, :], 0.0, "nt")
-        fill(T.et[:, :], 0.0, "et")
-        for b in range(4):
-            ts(T.et[:, 512 * b + b:512 * b + 512:4], T.rowi[:, :], T.pcol[:, :], 0.25, A.is_equal, A.mult,
-               ["rowi", "pcol"], ["et"])
-        quant("eq", "eqs", 0, 512, "et", 0, ["et"], ["eq"])
+        quant("wq", "ws", 0, 128, "wt", 0, ["wt"], ["wq"])
+        quant("adm", "adms", 0, 128, "zt", 0, ["zt0"], ["adm", "adms"])
+        quant("land0", "lans0", 512, 768, "zt", 0, ["zt0", "zt1"], ["lz0"])
 
     XQ, CQ, EQ = ("xq", "xs"), ("cq", "cqs"), ("eq", "eqs")
     for t in range(R):
         ca, cas = "ca%d" % t, "cas%d" % t
         CA = (ca, cas)
-        lm, meta = T["lm%d" % t], T["meta%d" % t]
+        lm, meta, yo, ido = T["lm%d" % t], T["meta%d" % t], T["yo%d" % t], T["ido%d" % t]
         land, lans, snd, sns = "land%d" % t, "lans%d" % t, "snd%d" % t, "sns%d" % t
         mm(0, 128, XQ, 192 * t, CA, 0, ["xq%d" % t, ca, cas])
         mm(1, 128, XQ, 192 * t + 64, CA, 0, ["xq%d" % t, ca, cas])
@@ -395,53 +384,70 @@ def rank_program(g, core, T, topo):
         slots("c", 2)
         send_codes(2)
         slots("c", 3)
-        if t == 0:
-            late_constants()
-        for h in range(2):
-            tt(T.vv[:, 16 * h:16 * h + 4], meta[:, 4 * rank:4 * rank + 4], T.cv[:, 16 * h:16 * h + 4], A.add,
-               [mk, "cv"], ["vvo%d" % h])
         for b in range(4):
             mm(4 + b, 128, EQ, 128 * b, CA, 0, ["eq", ca, cas])
         for b in range(4):
             run("s", lambda e: e.activation(T.hc[:, 32 * b:32 * b + 32], ps(4 + b, G * rank, G * rank + G), AF.Copy, scale=2.0),
                 ["ps%d" % (4 + b)], ["hc%d" % b])
         if t == 0:
-            quant("xq", "xs", 192, 384, "xt", 768, ["xt1"], ["xq1"])
-            quant("wq", "ws", 0, 128, "wt", 0, ["wt"], ["wq"])
-        if t == 1:
-            quant("xq", "xs", 384, 576, "xt", 1536, ["xt2"], ["xq2"])
-        if t < 2:
-            quant("land%d" % (t + 1), "lans%d" % (t + 1), 512, 768, "zt", 0, ["zt"], ["lz%d" % (t + 1)])
+            late_constants()
+        for h in range(2):
+            tt(T.vv[:, 16 * h:16 * h + 4], meta[:, 4 * rank:4 * rank + 4], T.cv[:, 16 * h:16 * h + 4], A.add,
+               [mk, "cv"], ["vvo%d" % h])
         arrive("arm%d" % t, n_meta, ["lm%d" % t])
         for h in range(2):
             tt(T.vv[:, 16 * h + 4:16 * h + 16], lm[:, :], T.cv[:, 16 * h + 4:16 * h + 16], A.add, ["lm%d" % t, "cv"], ["vvr%d" % h])
         VV = ["vvo0", "vvo1", "vvr0", "vvr1"]
-        run("v", lambda e: e.tensor_tensor_scan(T.pm[:, :], T.rsa[:, :], T.vv[:, :], FAR, A.max, A.min), VV + ["rsa"], ["pm"])
-        tt(T.mx[:, 1:32], T.vv[:, 1:32], T.pm[:, 0:31], A.max, VV + ["pm"], ["mx"])
-        ts(T.alst[:, 0:2], T.pm[:, 15:32:16], 1.0 / 512, None, A.mult, None, ["pm"], ["alst0"])
-        run("v", lambda e: e.tensor_tensor_scan(T.sc[:, 1:32], T.rsb[:, 1:32], T.mx[:, 1:32], FAR, A.max, A.min),
+        run("v", lambda e: e.tensor_tensor_scan(T.pmsc[:, 0:32], T.rsa[:, :], T.vv[:, :], FAR, A.max, A.min), VV + ["rsa"], ["pm"])
+        tt(T.mx[:, 1:32], T.vv[:, 1:32], T.pmsc[:, 0:31], A.max, VV + ["pm"], ["mx"])
+        run("v", lambda e: e.tensor_tensor_scan(T.pmsc[:, 33:64], T.rsb[:, 1:32], T.mx[:, 1:32], FAR, A.max, A.min),
             ["mx", "rsb"], ["sc"])
         for h in range(2):
-            c = T.sc[:, 15 + 16 * h:16 + 16 * h]
+            c = T.pmsc[:, 47 + 16 * h:48 + 16 * h]
             ts(T.sz[:, h:h + 1], c, BIG, c, A.is_lt, A.mult, ["sc"], ["sz%d" % h])
-        ts(T.alst[:, 2:4], T.sc[:, 15:32:16], 1.0 / 512, None, A.mult, None, ["sc"], ["alst1"])
+        FS = T.pmsc[:, 15:64:16]
+        ts(T.alst[:, 0:4], FS, 1.0 / 512, None, A.mult, None, ["pm", "sc"], ["alst0"])
         for h in range(2):
-            ts(T.alst[:, 4 + h:5 + h], T.sz[:, h:h + 1], T.pm[:, 15 + 16 * h:16 + 16 * h], 1.0 / 512, A.max, A.mult,
-               ["sz%d" % h, "pm"], ["alst%d" % (2 + h)])
+            ts(T.alst[:, 4 + h:5 + h], T.sz[:, h:h + 1], T.pmsc[:, 15 + 16 * h:16 + 16 * h], 1.0 / 512, A.max, A.mult,
+               ["sz%d" % h, "pm"], ["alst%d" % (1 + h)])
+
+        def numbers1():
+            run("v", lambda e: e.tensor_copy(T.vi[:, :], FS), ["pm", "sc"], ["vi"])
+            ts(T.val[:, :], FS, BIG, None, A.is_lt, None, ["pm", "sc"], ["val"])
+            ts(T.sv[:, :], T.vi[:, :], 15, None, A.arith_shift_right, None, ["vi"], ["sv"])
+            ts(T.iv[:, :], T.vi[:, :], 511, None, A.bitwise_and, None, ["vi"], ["iv"])
+            ts(T.s192[:, :], T.sv[:, :], float(TOK), 1.0, A.mult, A.add, ["sv"], ["s192"])
+
+        def numbers2():
+            tt(T.idf[:, :], T.s192[:, :], T.iv[:, :], A.add, ["s192", "iv"], ["idf"])
+            tt(T.idg[:, :], T.idf[:, :], T.val[:, :], A.mult, ["idf", "val"], ["idg"])
+            for i in range(2):
+                ts(ido[:, i:4:2], T.idg[:, 2 * i:2 * i + 2], -1.0, None, A.add, None, ["idg"], ["ido%d%d" % (t, i)])
+            for h in range(2):
+                dma("y", T.ids[0:1, 64 * t + 32 * h:64 * t + 32 * h + 32], ido[0:16, 2 * h:2 * h + 2],
+                    ["ido%d0" % t, "ido%d1" % t], [], "st")
+        last = t == R - 1
+        if last:
+            numbers1()
         arrive("ark%d" % t, n_tok, [land, lans])
-        AL = ["alst0", "alst1", "alst2", "alst3", "lz%d" % t]
+        AL = ["alst0", "alst1", "alst2", "lz%d" % t]
         pick("c", "adm", 0, 96, land, 0, 768, "alst", 0, AL + [land], ["adm"])
         pick("s", "adms", 0, 96, lans, 0, 768, "alst", 0, AL + [lans], ["adms"])
         for b in range(4):
             mm(b, 128, EQ, 128 * b, ("adm", "adms"), 0, ["eq", "adm", "adms"])
         mm(6, 128, ("wq", "ws"), 0, ("adm", "adms"), 0, ["wq", "adm", "adms"])
-        ts(T.mv[:, :], T.pm[:, 15:32:16], BIG, float(G * rank - 128), A.is_ge, A.mult, ["pm"], ["mv"])
+        ts(T.mv[:, :], T.pmsc[:, 15:32:16], BIG, float(G * rank - 128), A.is_ge, A.mult, ["pm"], ["mv"])
         for h in range(2):
             ts(T.clst[:, h:h + 1], T.mv[:, h:h + 1], T.gnew[:, h:h + 1], None, A.add, None, ["mv", "gnew%d" % h], ["clst%d" % h])
         if t == 0:
             await_("v", writers["nt"])
         for b in range(4):
             run("s", lambda e: e.activation(T.s4[:, 32 * b:32 * b + 32], ps(b, 64, 96), AF.Copy), ["ps%d" % b], ["s4%d" % b])
+        for i in range(2):
+            run("s", lambda e: e.activation(yo[:, i:64:2], ps(6, 32 * i, 32 * i + 32), AF.Copy), ["ps6"], ["yo%d%d" % (t, i)])
+        if last:
+            numbers2()
+        dma("y", T.y[:, 64 * t:64 * t + 64], yo[:, :], ["yo%d0" % t, "yo%d1" % t], [], "st")
         for b in range(5):
             if b < 4:
                 tt(T.hh[:, 32 * b:32 * b + 32], ps(b, 0, 32), T.s4[:, 32 * b:32 * b + 32], A.add, ["ps%d" % b, "s4%d" % b], ["hh%d" % b])
@@ -453,30 +459,17 @@ def rank_program(g, core, T, topo):
         CL = ["clst0", "clst1", ca + "n"]
         pick("c", cn, G * rank, G, ca, 0, 256, "clst", 0, CL + [ca], [cn])
         pick("s", cns, G * rank, G, cas, 0, 256, "clst", 0, CL + [cas], [cns])
-        if t < R - 1:
-            remote([many(T[cn][:, own].bitcast(dt.uint8), T[cn][:, own].bitcast(dt.uint8), "arc%d" % (t + 1))], [cn])
-            remote([many(T[cns][:, own], T[cns][:, own], "arc%d" % (t + 1))], [cns])
-        else:
+        if last:
             dma("y", T.oc[:, :], T[cn][:, own].bitcast(dt.uint8), [cn], [], "st")
             for k in range(4):
                 dma("y" if k % 2 else "s", T.osc[4 * k:4 * k + 4, :], T[cns][32 * k:32 * k + 4, own], [cns], [], "st")
-        yo, ido = T["yo%d" % t], T["ido%d" % t]
-        for i in range(2):
-            run("s", lambda e: e.activation(yo[:, i:64:2], ps(6, 32 * i, 32 * i + 32), AF.Copy), ["ps6"], ["yo%d%d" % (t, i)])
-        dma("y", T.y[:, 64 * t:64 * t + 64], yo[:, :], ["yo%d0" % t, "yo%d1" % t], [], "st")
-        cp("v", T.vi[:, 0:4:2], T.pm[:, 15:32:16], ["pm"], ["vi0"])
-        cp("v", T.vi[:, 1:4:2], T.sc[:, 15:32:16], ["sc"], ["vi1"])
-        VI = ["vi0", "vi1"]
-        ts(T.sv[:, :], T.vi[:, :], 15, None, A.arith_shift_right, None, VI, ["sv"])
-        ts(T.iv[:, :], T.vi[:, :], 511, None, A.bitwise_and, None, VI, ["iv"])
-        ts(T.val[:, :], T.vi[:, :], BIG, None, A.is_lt, None, VI, ["val"])
-        ts(T.s192[:, :], T.sv[:, :], float(TOK), 1.0, A.mult, A.add, ["sv"], ["s192"])
-        tt(T.idf[:, :], T.s192[:, :], T.iv[:, :], A.add, ["s192", "iv"], ["idf"])
-        tt(T.idg[:, :], T.idf[:, :], T.val[:, :], A.mult, ["idf", "val"], ["idg"])
-        ts(ido[:, :], T.idg[:, :], -1.0, None, A.add, None, ["idg"], ["ido%d" % t])
-        for h in range(2):
-            dma("y", T.ids[0:1, 64 * t + 32 * h:64 * t + 32 * h + 32], ido[0:16, 2 * h:2 * h + 2], ["ido%d" % t], [], "st")
-        if t < R - 1:
+        else:
+            remote([many(T[cn][:, own].bitcast(dt.uint8), T[cn][:, own].bitcast(dt.uint8), "arc%d" % (t + 1))], [cn])
+            remote([many(T[cns][:, own], T[cns][:, own], "arc%d" % (t + 1))], [cns])
+            quant("xq", "xs", 192 * t + 192, 192 * t + 384, "xt", 768 * t + 768, ["xt%d" % (t + 1)], ["xq%d" % (t + 1)])
+            numbers1()
+            numbers2()
+            quant("land%d" % (t + 1), "lans%d" % (t + 1), 512, 768, "zt", 0, ["zt0", "zt1"], ["lz%d" % (t + 1)])
             arrive("arc%d" % (t + 1), n_cen, [cn, cns])
     for k in cnt:
         if know["p"].get(k, 0) < cnt[k]:

@@ -3,40 +3,43 @@ from concourse.mybir import dt, AluOpType as A, ActivationFunctionType as AF
 
 CODE = "float8_e4m3fn_x4"
 N, G, TOK, R, CAPP = 4, 32, 192, 3, 64
-BIG = 262144.0
-PEN = 524288.0
-FAR = 1.0e9
+UNIT = 2.0 ** -18
+WIN = 512
+FAR = 64.0
 LOW = -1.0e29
+LIFT = 1024.0
 
 SCRATCH = {
-    "cbt": ("sbuf", [128, 512], "bfloat16"), "xt": ("sbuf", [128, 2304], "bfloat16"), "wt": ("sbuf", [128, 512], "bfloat16"),
-    "zt": ("sbuf", [128, 1024], "bfloat16"), "pt": ("sbuf", [128, 528], "bfloat16"), "zz": ("sbuf", [128, 528], "bfloat16"),
+    "cbt": ("sbuf", [128, 768], "bfloat16"), "xt": ("sbuf", [128, 2304], "bfloat16"), "wt": ("sbuf", [128, 512], "bfloat16"),
+    "pt": ("sbuf", [128, 512], "bfloat16"), "zz": ("sbuf", [128, 512], "bfloat16"),
+    "ptx": ("sbuf", [128, 512], "bfloat16"), "zzx": ("sbuf", [128, 512], "bfloat16"),
     "nt": ("sbuf", [128, 512], "bfloat16"), "ct": ("sbuf", [128, 2048], "bfloat16"), "et": ("sbuf", [128, 2048], "bfloat16"),
-    "idg": ("sbuf", [128, 4], "float32"), "ps": ("psum", [128, 4096], "float32"),
+    "idf": ("sbuf", [128, 4], "float32"), "ps": ("psum", [128, 4096], "float32"),
 }
 for _c, _s, _n in (("cq", "cqs", 512), ("eq", "eqs", 512), ("cbq", "cbs", 128), ("xq", "xs", 576), ("wq", "ws", 128),
-                   ("pq", "pqs", 132), ("zq", "zqs", 132), ("adm", "adms", 128)):
+                   ("pq", "pqs", 128), ("zq", "zqs", 128), ("pxq", "pxs", 128), ("zxq", "zxs", 128), ("adm", "adms", 160),
+                   ("ady", "adys", 128)):
     SCRATCH[_c] = ("sbuf", [128, _n], CODE)
     SCRATCH[_s] = ("sbuf", [128, _n], "uint8")
-for _b in ("rowi", "k16", "negc", "ma", "mb", "msk", "msk2", "ls1", "ls2", "s4", "hh", "hc"):
+for _b in ("rowi", "k16", "negc", "ma", "mb", "msk", "ls1", "ls2", "dist", "hc", "s4", "hh"):
     SCRATCH[_b] = ("sbuf", [128, 128], "float32")
-for _b in ("pcol", "qcol", "qcol1", "corr", "ncorr"):
+for _b in ("pcol", "npcol", "qcol", "corr", "ncorr"):
     SCRATCH[_b] = ("sbuf", [128, 1], "float32")
-for _b in ("offi", "pen", "cv", "vv", "mx", "rsa", "rsb"):
+for _b in ("dd", "ab", "mx", "sec", "junk"):
     SCRATCH[_b] = ("sbuf", [128, 32], "float32")
-SCRATCH["pmsc"] = ("sbuf", [128, 64], "float32")
-for _b, _n, _d in (("pi", 1, "int32"), ("qi", 1, "int32"), ("ii", 16, "float32"), ("tt", 16, "float32"), ("lst", 16, "uint16"),
-                   ("sz", 2, "float32"), ("alst", 6, "uint16"), ("mv", 2, "float32"), ("clst", 2, "uint16"),
+for _b, _n, _d in (("pi", 1, "int32"), ("qi", 1, "int32"), ("ii", 16, "float32"), ("hold", 16, "float32"), ("cut", 16, "float32"),
+                   ("flag", 16, "float32"), ("lst", 16, "uint16"), ("cs", 2, "float32"), ("v2", 2, "float32"),
+                   ("f5", 2, "float32"), ("alst", 6, "uint16"), ("mv", 2, "float32"), ("clst", 2, "uint16"),
                    ("ilst", 2, "uint16"), ("gnew", 2, "float32"), ("vi", 4, "int32"), ("iv", 4, "int32"), ("sv", 4, "int32"),
-                   ("s192", 4, "float32"), ("idf", 4, "float32"), ("val", 4, "float32")):
+                   ("s192", 4, "float32"), ("sg", 4, "float32"), ("wv", 4, "float32")):
     SCRATCH[_b] = ("sbuf", [128, _n], _d)
 for _t in range(R):
     SCRATCH["meta%d" % _t] = ("sbuf", [128, 16], "bfloat16")
-    SCRATCH["lm%d" % _t] = ("sbuf", [128, 12], "bfloat16")
+    SCRATCH["lm%d" % _t] = ("sbuf", [128, 20], "bfloat16")
     SCRATCH["snd%d" % _t] = ("sbuf", [128, 192], CODE)
     SCRATCH["sns%d" % _t] = ("sbuf", [128, 192], "uint8")
-    SCRATCH["land%d" % _t] = ("sbuf", [128, 768], CODE)
-    SCRATCH["lans%d" % _t] = ("sbuf", [128, 768], "uint8")
+    SCRATCH["land%d" % _t] = ("sbuf", [128, 640], CODE)
+    SCRATCH["lans%d" % _t] = ("sbuf", [128, 640], "uint8")
     SCRATCH["yo%d" % _t] = ("sbuf", [128, 64], "float32")
     SCRATCH["ido%d" % _t] = ("sbuf", [128, 4], "float32")
 for _t in range(R + 1):
@@ -171,20 +174,30 @@ def rank_program(g, core, T, topo):
     def tt(out, a, b, op, rd, wr):
         run("v", lambda e: e.tensor_tensor(out, a, b, op), rd, wr)
 
+    def scan(out, a, b, first, o0, o1, rd, wr):
+        run("v", lambda e: e.tensor_tensor_scan(out, a, b, first, o0, o1), rd, wr)
+
+    def act(out, in_, func, bias, scale, rd, wr, total=None):
+        run("s", lambda e: e.activation(out, in_, func, bias=bias, scale=scale, accum_out=total), rd, wr)
+
     def fill(ap, c, key):
         run("v", lambda e: e.memset(ap, c), [], [key])
 
     def flat(out, in_, c, rd, key):
-        run("s", lambda e: e.activation(out, in_, AF.Identity, bias=c, scale=0.0), rd, [key])
+        act(out, in_, AF.Identity, c, 0.0, rd, [key])
 
     def quant(c, s, a, b, tile, x, keys, out):
         run("v", lambda e: e.quantize_mx(T[c][:, a:b], T[s][:, a:b], T[tile][:, x:x + 4 * (b - a)]), keys, out)
 
-    def mm(bank, n, l, la, r, ra, rd):
+    def mm(bank, l, la, r, ras, rd):
         lc, lsc = l
         rc, rs = r
-        run("t", lambda e: e.matmul_mx(T.ps[:, 512 * bank:512 * bank + n], T[lc][:, la:la + 128], T[lsc][:, la:la + 128],
-                                       T[rc][:, ra:ra + n], T[rs][:, ra:ra + n], True, True), rd, ["ps%d" % bank])
+        await_("t", deps("t", rd, ["ps%d" % bank]))
+        for i, ra in enumerate(ras):
+            call = g.tensor.matmul_mx(T.ps[:, 512 * bank:512 * bank + 128], T[lc][:, la:la + 128], T[lsc][:, la:la + 128],
+                                      T[rc][:, ra:ra + 128], T[rs][:, ra:ra + 128], i == 0, i == len(ras) - 1)
+        call.then_inc(T.sem["qt"], 1)
+        note(record("t", "qt", 1), rd, ["ps%d" % bank])
 
     def pick(kind, dstb, da, n, srcb, sa, sb, lstb, la, rd, wr):
         k = n // 16
@@ -205,31 +218,22 @@ def rank_program(g, core, T, topo):
         return T.ps[p0:128, 512 * bank + a:512 * bank + b]
 
     dma("y", T.cbt[:, 0:128], T.cb[:, :], [], ["cbt"], "ldcb")
-    dma("s", T.xt[:, 0:768], T.x[:, 0:768], [], ["xt0"], "ldx0")
-    dma("y", T.xt[:, 768:1536], T.x[:, 768:1536], [], ["xt1"], "ldx1")
-    dma("y", T.wt[:, :], T.w[:, :], [], ["wt"], "ldw")
-    dma("y", T.xt[:, 1536:2304], T.x[:, 1536:2304], [], ["xt2"], "ldx2")
+    dma("y", T.xt[:, 0:768], T.x[:, 0:768], [], ["xt0"], "ldx0")
 
     iota(T.pi[:, :], [[1, 1]], 0, 1, "pi", False)
     iota(T.rowi[:, :], [[1, 128]], 0, 0, "rowi")
     iota(T.pcol[:, :], [[1, 1]], 0, 1, "pcol")
+    iota(T.npcol[:, :], [[1, 1]], 0, -1, "npcol")
     iota(T.k16[:, :], [[0, 8], [1, 16]], 0, 0, "k16")
-    for t in range(4):
-        flat(T.ct[:, 1024 + t:1536:4], T.rowi[:, :], 1.0 if t < 2 else 0.0, ["rowi"], "ct1024%d" % t)
-        flat(T.ct[:, 1536 + t:2048:4], T.rowi[:, :], -1.0 if t < 2 else 1.0, ["rowi"], "ct1536%d" % t)
-    flat(T.ct[:, 3:512:4], T.rowi[:, :], 0.0, ["rowi"], "ct0d")
-    flat(T.ct[:, 512:1024:4], T.rowi[:, :], 1.0, ["rowi"], "ct512a")
-    flat(T.ct[:, 514:1024:4], T.rowi[:, :], -1.0, ["rowi"], "ct512b")
-    fill(T.cbt[:, 128:512], 0.0, "cbtz")
-    fill(T.pt[:, :], 0.0, "pt")
+    fill(T.et[:, :], 0.0, "etz")
+    fill(T.cbt[:, 128:768], 0.0, "cbtz")
     ts(T.qi[:, :], T.pi[:, :], 15, None, A.bitwise_and, None, ["pi"], ["qi"])
-    fill(T.negc[:, :], LOW, "negc")
     run("v", lambda e: e.tensor_copy(T.qcol[:, :], T.qi[:, :]), ["qi"], ["qcol"])
-    fill(T.ct[64:128, 1:512:4], 0.0, "ct0c")
     for h in range(2):
         ts(T.ilst[:, h:h + 1], T.qcol[:, :], 16.0 * h, None, A.add, None, ["qcol"], ["ilst%d" % h])
-    ts(T.ct[:, 0:512:4], T.rowi[:, :], T.pcol[:, :], None, A.is_ge, None, ["rowi", "pcol"], ["ct0a"])
-    ts(T.ct[:, 2:512:4], T.rowi[:, :], T.pcol[:, :], -1.0, A.is_ge, A.mult, ["rowi", "pcol"], ["ct0b"])
+    for key, sl, c in (("ct0c", slice(1, 512, 4), 0.0), ("ct0d", slice(3, 512, 4), 0.0), ("ct1a", slice(512, 1024, 4), 1.0),
+                       ("ct1b", slice(514, 1024, 4), -1.0)):
+        flat(T.ct[:, sl], T.rowi[:, :], c, ["rowi"], key)
 
     quant("cbq", "cbs", 0, 128, "cbt", 0, ["cbt", "cbtz"], ["cbq"])
     own = slice(G * rank, G * rank + G)
@@ -238,115 +242,105 @@ def rank_program(g, core, T, topo):
     pick("c", "ca0", G * rank, G, "cbq", 0, 128, "ilst", 0, ["cbq", "ilst0", "ilst1"], ["ca0"])
     pick("s", "cas0", G * rank, G, "cbs", 0, 128, "ilst", 0, ["cbq", "ilst0", "ilst1"], ["cas0"])
     arrive("arc0", n_cen, ["ca0", "cas0"])
-    quant("xq", "xs", 0, 192, "xt", 0, ["xt0"], ["xq0"])
-    order = [rank] + [s for s in range(N) if s != rank]
-    for h in range(2):
-        for e, s in enumerate(order):
-            iota(T.offi[:, 16 * h + 4 * e:16 * h + 4 * e + 4], [[16, 4]], 64 * s, 0, "offi%d%d" % (h, e))
-        iota(T.pen[:, 16 * h:16 * h + 16], [[0, 4], [1 - 2 * h, 2], [0, 2]], h, 0, "pen%d" % h)
-    offk = ["offi%d%d" % (h, e) for h in range(2) for e in range(4)]
-
-    ts(T.ct[64:128, 513:1024:4], T.rowi[64:128, :], T.pcol[64:128, :], None, A.is_ge, None, ["rowi", "pcol"], ["ct512c"])
-    ts(T.ct[64:128, 515:1024:4], T.rowi[64:128, :], T.pcol[64:128, :], -1.0, A.is_ge, A.mult, ["rowi", "pcol"], ["ct512d"])
-    fill(T.ct[0:64, 1:512:4], -1.0, "ct0e")
-    fill(T.ct[0:64, 513:1024:4], -1.0, "ct512e")
-    fill(T.ct[0:64, 515:1024:4], 0.0, "ct512f")
-    quant("cq", "cqs", 0, 512, "ct", 0, ["ct0a", "ct0b", "ct0c", "ct0d", "ct0e", "ct512a", "ct512b", "ct512c", "ct512d",
-                                         "ct512e", "ct512f"] + ["ct1024%d" % t for t in range(4)]
-          + ["ct1536%d" % t for t in range(4)], ["cq"])
+    iota(T.ptx[:, :], [[0, 512]], 0, 0, "ptx")
+    iota(T.zzx[:, :], [[0, 512]], 0, 0, "zzx")
+    iota(T.hold[:, :], [[0, 4], [1, 4]], 0, 0, "hold")
+    for i, c in enumerate((1.0, 1.0, 0.0, 0.0)):
+        flat(T.ct[:, 1024 + i:1536:4], T.rowi[:, :], c, ["rowi"], "ct2%d" % i)
+    fill(T.negc[:, :], LOW, "negc")
+    ts(T.ct[:, 0:512:4], T.rowi[:, :], T.pcol[:, :], None, A.is_ge, None, ["rowi", "pcol"], ["ct0a"])
+    ts(T.ct[:, 2:512:4], T.rowi[:, :], T.pcol[:, :], -1.0, A.is_ge, A.mult, ["rowi", "pcol"], ["ct0b"])
+    for i, c in enumerate((0.0, -1.0, 1.0, 1.0)):
+        fill(T.ct[:, 1536 + i:2048:4], c, "ct3%d" % i)
+    ts(T.ct[64:128, 513:1024:4], T.rowi[64:128, :], T.pcol[64:128, :], None, A.is_ge, None, ["rowi", "pcol"], ["ct1c"])
+    ts(T.ct[64:128, 515:1024:4], T.rowi[64:128, :], T.pcol[64:128, :], -1.0, A.is_ge, A.mult, ["rowi", "pcol"], ["ct1d"])
+    fill(T.ct[0:64, 513:1024:4], 0.0, "ct1e")
+    fill(T.ct[0:64, 515:1024:4], 0.0, "ct1f")
+    fill(T.pt[:, :], 0.0, "pt")
+    fill(T.zz[0:64, 1:512:4], 0.0, "zza")
+    fill(T.zz[0:64, 3:512:4], 0.0, "zzb")
     fill(T.pt[:, 0:1], 1.0, "pt")
     fill(T.pt[64:128, 1:2], 1.0, "pt")
-    fill(T.pt[:, 512:513], 1.0, "pt")
-    fill(T.pt[64:128, 513:514], 1.0, "pt")
-    fill(T.pt[0:64, 513:528:4], 1.0, "pt")
-    fill(T.zz[:, :], 0.0, "zz")
-    ts(T.qcol1[:, :], T.qcol[:, :], 1.0, None, A.add, None, ["qcol"], ["qcol1"])
-    ts(T.corr[:, :], T.qcol[:, :], 15.0, 1024.0, A.is_lt, A.mult, ["qcol"], ["corr"])
-    ts(T.msk[:, :], T.k16[:, :], T.qcol[:, :], -4096.0, A.is_equal, A.mult, ["k16", "qcol"], ["msk"])
-    ts(T.msk2[:, :], T.k16[:, :], T.qcol1[:, :], 1024.0, A.is_equal, A.mult, ["k16", "qcol1"], ["msk2"])
-    ts(T.ncorr[:, :], T.corr[:, :], -1.0, None, A.mult, None, ["corr"], ["ncorr"])
-    tt(T.msk[:, :], T.msk[:, :], T.msk2[:, :], A.add, ["msk2"], ["msk"])
+    quant("cq", "cqs", 0, 512, "ct", 0, ["ct0a", "ct0b", "ct0c", "ct0d", "ct1a", "ct1b", "ct1c", "ct1d", "ct1e", "ct1f"]
+          + ["ct%d%d" % (b, i) for b in (2, 3) for i in range(4)], ["cq"])
+    ts(T.msk[:, :], T.k16[:, :], T.qcol[:, :], -33.0 * LIFT, A.is_equal, A.mult, ["k16", "qcol"], ["msk"])
+    ts(T.corr[:, :], T.qcol[:, :], -LIFT, 15.0 * LIFT, A.mult, A.add, ["qcol"], ["corr"])
+    quant("xq", "xs", 0, 192, "xt", 0, ["xt0"], ["xq0"])
+    ts(T.msk[:, :], T.msk[:, :], LIFT, None, A.add, None, [], ["msk"])
+    ts(T.ncorr[:, :], T.corr[:, :], -UNIT, None, A.mult, None, ["corr"], ["ncorr"])
+    fill(T.ptx[:, 0:1], 1.0, "ptx")
+    fill(T.ptx[64:128, 1:2], 1.0, "ptx")
+    act(T.dist[:, :], T.rowi[:, :], AF.Abs, T.npcol[:, 0:1], 1.0, ["rowi", "npcol"], ["dist"])
     for b in range(4):
-        flat(T.et[:, 512 * b:512 * b + 512], T.cbt[:, :], 0.0, ["cbt", "cbtz"], "et%d" % b)
-    for b in range(4):
-        ts(T.et[:, 512 * b + b:512 * b + 512:4], T.rowi[:, :], T.pcol[:, :], 0.25, A.is_equal, A.mult,
-           ["rowi", "pcol"], ["et%d" % b])
-    quant("eq", "eqs", 0, 512, "et", 0, ["et%d" % b for b in range(4)], ["eq"])
+        act(T.et[:, 512 * b + b:512 * b + 512:4], T.dist[:, :], AF.Relu, 0.25, -0.25, ["dist", "etz"], ["et%d" % b])
+    await_("y", writers["ca0"])
+    dma("y", T.wt[:, :], T.w[:, :], [], ["wt"], "ldw")
+    dma("y", T.xt[:, 768:1536], T.x[:, 768:1536], [], ["xt1"], "ldx1")
+
+    def zero_block(t):
+        quant("land%d" % t, "lans%d" % t, WIN, WIN + 128, "cbt", 128, ["cbtz"], ["lz%d" % t])
 
     def late_constants():
-        for b in range(2):
-            flat(T.zt[:, 512 * b:512 * b + 512], T.cbt[:, :], 0.0, ["cbt", "cbtz"], "zt%d" % b)
-        flat(T.nt[:, :], T.cbt[:, :], 0.0, ["cbt", "cbtz"], "nt")
-        ts(T.cv[:, :], T.offi[:, :], T.qcol[:, :], 512.0, A.add, A.mult, offk + ["qcol"], ["cv"])
-        ts(T.pen[:, :], T.pen[:, :], PEN, None, A.mult, None, [], ["pen0", "pen1"])
-        fill(T.rsa[:, :], -FAR, "rsa")
-        tt(T.cv[:, :], T.cv[:, :], T.pen[:, :], A.add, ["pen0", "pen1"], ["cv"])
-        fill(T.rsb[:, :], -FAR, "rsb")
-        fill(T.rsa[:, 16:17], FAR, "rsa")
-        fill(T.rsb[:, 17:18], FAR, "rsb")
+        flat(T.nt[:, :], T.cbt[:, 128:640], 0.0, ["cbtz"], "nt")
         for h in range(2):
             ts(T.gnew[:, h:h + 1], T.qcol[:, :], 128.0 + 16 * h, None, A.add, None, ["qcol"], ["gnew%d" % h])
-        quant("wq", "ws", 0, 128, "wt", 0, ["wt"], ["wq"])
-        quant("adm", "adms", 0, 128, "zt", 0, ["zt0"], ["adm", "adms"])
-        quant("land0", "lans0", 512, 768, "zt", 0, ["zt0", "zt1"], ["lz0"])
+        quant("adm", "adms", 0, 160, "cbt", 128, ["cbtz"], ["adm", "adms"])
+        zero_block(0)
 
     XQ, CQ, EQ = ("xq", "xs"), ("cq", "cqs"), ("eq", "eqs")
     for t in range(R):
+        last = t == R - 1
         ca, cas = "ca%d" % t, "cas%d" % t
         CA = (ca, cas)
         lm, meta, yo, ido = T["lm%d" % t], T["meta%d" % t], T["yo%d" % t], T["ido%d" % t]
         land, lans, snd, sns = "land%d" % t, "lans%d" % t, "snd%d" % t, "sns%d" % t
-        mm(0, 128, XQ, 192 * t, CA, 0, ["xq%d" % t, ca, cas])
-        mm(1, 128, XQ, 192 * t + 64, CA, 0, ["xq%d" % t, ca, cas])
-        for bank, m, p0 in ((0, T.ma, 0), (1, T.mb, 64)):
-            key = "ma" if bank == 0 else "mb"
-            run("v", lambda e: e.tensor_tensor_scan(m[p0:128, :], ps(bank, 0, 128, p0), T.negc[p0:128, :], LOW, A.max, A.max),
-                ["ps%d" % bank, "negc"], [key])
+        mm(0, XQ, 192 * t, CA, (0,), ["xq%d" % t, ca, cas])
+        mm(1, XQ, 192 * t + 64, CA, (0,), ["xq%d" % t, ca, cas])
+        scan(T.ma[:, :], ps(0, 0, 128), T.negc[:, :], LOW, A.max, A.max, ["ps0", "negc"], ["ma"])
+        scan(T.mb[64:128, :], ps(1, 0, 128, 64), T.negc[64:128, :], LOW, A.max, A.max, ["ps1", "negc"], ["mb"])
 
-        def before(q, m, key, p0, el, k0, k1, step, oc, wr):
-            n = len(range(k0, k1, step))
-            out = T.pt[p0:128, 4 * oc + el:min(4 * (oc + n), 528):4]
+        def before(q, out, m, key, p0, k0, k1, step, wr):
             if q == "v":
                 ts(out, m[p0:128, k0:k1:step], m[p0:128, 127:128], None, A.is_lt, None, [key], [wr])
             else:
-                run("s", lambda e: e.activation(out, m[p0:128, k0:k1:step], AF.Sign, bias=m[p0:128, 127:128], scale=-1.0),
-                    [key], [wr])
+                act(out, m[p0:128, k0:k1:step], AF.Sign, m[p0:128, 127:128], -1.0, [key], [wr])
         if t == 0:
-            await_("s", writers["pt"] + writers["zz"])
-            await_("v", writers["pt"] + writers["zz"])
-        before("s", T.ma, "ma", 0, 0, 0, 127, 1, 1, "pt0")
-        before("s", T.ma, "ma", 0, 2, 0, 128, 1, 0, "pt2")
-        before("s", T.ma, "ma", 0, 0, 31, 96, 32, 129, "pt0x")
-        before("s", T.ma, "ma", 0, 2, 31, 128, 32, 128, "pt2x")
-        before("v", T.mb, "mb", 64, 1, 0, 127, 1, 1, "pt1")
-        before("v", T.mb, "mb", 64, 3, 0, 128, 1, 0, "pt3")
-        before("s", T.mb, "mb", 64, 1, 31, 96, 32, 129, "pt1x")
-        before("v", T.mb, "mb", 64, 3, 31, 128, 32, 128, "pt3x")
-        quant("pq", "pqs", 0, 132, "pt", 0, ["pt", "pt0", "pt1", "pt2", "pt3", "pt0x", "pt1x", "pt2x", "pt3x"], ["pq"])
-        mm(2, 132, CQ, 0, ("pq", "pqs"), 0, ["cq", "pq"])
-        mm(3, 132, CQ, 128, ("pq", "pqs"), 0, ["cq", "pq"])
-
-        def below1(bank, p0, el, wr):
-            ts(T.zz[p0:128, el:528:4], ps(bank, 0, 132, p0), 1.0, None, A.is_lt, None, ["ps%d" % bank], [wr])
-
-        def below2(bank, p0, el, wr):
-            run("s", lambda e: e.activation(T.zz[p0:128, el:512:4], ps(bank, 0, 128, p0), AF.Relu, bias=2.0, scale=-1.0),
-                ["ps%d" % bank], [wr])
-        below1(2, 0, 0, "zz0")
-        below2(3, 64, 3, "zz3")
-        below1(3, 64, 1, "zz1")
-        below2(2, 0, 2, "zz2")
-        quant("zq", "zqs", 0, 132, "zz", 0, ["zz", "zz0", "zz1", "zz2", "zz3"], ["zq"])
-        mm(4, 132, CQ, 256, ("zq", "zqs"), 0, ["cq", "zq"])
-        mm(5, 132, CQ, 384, ("zq", "zqs"), 0, ["cq", "zq"])
+            await_("s", writers["pt"] + writers["ptx"])
+            await_("v", writers["pt"] + writers["ptx"])
+        before("s", T.pt[:, 4:512:4], T.ma, "ma", 0, 0, 127, 1, "pt0")
+        before("s", T.pt[:, 2:512:4], T.ma, "ma", 0, 0, 128, 1, "pt2")
+        before("v", T.pt[64:128, 5:512:4], T.mb, "mb", 64, 0, 127, 1, "pt1")
+        before("v", T.pt[64:128, 3:512:4], T.mb, "mb", 64, 0, 128, 1, "pt3")
+        before("v", T.ptx[64:128, 5:14:4], T.mb, "mb", 64, 31, 96, 32, "px1")
+        before("v", T.ptx[64:128, 3:12:4], T.mb, "mb", 64, 31, 96, 32, "px3")
+        quant("pq", "pqs", 0, 128, "pt", 0, ["pt", "pt0", "pt1", "pt2", "pt3"], ["pq"])
+        before("s", T.ptx[:, 4:13:4], T.ma, "ma", 0, 31, 96, 32, "px0")
+        before("s", T.ptx[:, 2:11:4], T.ma, "ma", 0, 31, 96, 32, "px2")
+        mm(3, CQ, 128, ("pq", "pqs"), (0,), ["cq", "pq"])
+        mm(2, CQ, 0, ("pq", "pqs"), (0,), ["cq", "pq"])
+        quant("pxq", "pxs", 0, 128, "ptx", 0, ["ptx", "px0", "px1", "px2", "px3"], ["pxq"])
+        mm(6, CQ, 0, ("pxq", "pxs"), (0,), ["cq", "pxq"])
+        mm(7, CQ, 128, ("pxq", "pxs"), (0,), ["cq", "pxq"])
+        for el, c in ((1, 1.0), (3, 2.0)):
+            act(T.zz[64:128, el:512:4], ps(3, 0, 128, 64), AF.Relu, c, -1.0, ["ps3"], ["zz%d" % el])
+        for el, c in ((0, 1.0), (2, 2.0)):
+            ts(T.zz[:, el:512:4], ps(2, 0, 128), c, None, A.is_lt, None, ["ps2"], ["zz%d" % el])
+        quant("zq", "zqs", 0, 128, "zz", 0, ["zza", "zzb", "zz0", "zz1", "zz2", "zz3"], ["zq"])
+        mm(4, CQ, 256, ("zq", "zqs"), (0,), ["cq", "zq"])
+        mm(5, CQ, 384, ("zq", "zqs"), (0,), ["cq", "zq"])
+        for el, bank, p0 in ((0, 6, 0), (1, 7, 64)):
+            ts(T.zzx[p0:128, el:64:16], ps(bank, 0, 4, p0), CAPP + 1.0, UNIT, A.is_lt, A.mult, ["ps%d" % bank, "zzx"], ["zx%d" % el])
+        quant("zxq", "zxs", 0, 128, "zzx", 0, ["zzx", "zx0", "zx1"], ["zxq"])
+        mm(0, CQ, 256, ("zxq", "zxs"), (0,), ["cq", "zxq"])
         for j, ls in ((0, T.ls1), (1, T.ls2)):
-            run("v", lambda e: e.tensor_tensor_scan(ls[:, :], T.msk[:, :], ps(4 + j, 0, 128), 0.0, A.add, A.max),
-                ["ps%d" % (4 + j), "msk"], ["ls%d" % j])
+            scan(ls[:, :], T.msk[:, :], ps(4 + j, 0, 128), 0.0, A.add, A.max, ["ps%d" % (4 + j), "msk"], ["ls%d" % j])
         for j, ls in ((0, T.ls1), (1, T.ls2)):
-            run("s", lambda e: e.activation(T.ii[:, j:16:2], ls[:, 15:128:16], AF.Identity, bias=T.ncorr[:, 0:1], scale=1.0),
-                ["ls%d" % j, "ncorr"], ["ii%d" % j])
+            for h in range(2):
+                act(T.ii[:, 2 * j + h:16:4], ls[:, 15 + 16 * h:128:32], AF.Identity, T.ncorr[:, 0:1], UNIT, ["ls%d" % j, "ncorr"],
+                    ["ii%d%d" % (j, h)])
             ts(T.lst[:, j:16:2], ls[:, 15:128:16], T.corr[:, 0:1], float(TOK - 1), A.subtract, A.min,
                ["ls%d" % j, "corr"], ["lst%d" % j])
+        II = ["ii00", "ii01", "ii10", "ii11"]
         LST = ["lst0", "lst1"]
         mk = "meta%d" % t
         sp0, sp1 = split(rank, 0), split(rank, 1)
@@ -367,93 +361,117 @@ def rank_program(g, core, T, topo):
 
         def place(d):
             e = [s for s in range(N) if s != d].index(rank)
-            return slice(4 * e, 4 * e + 4)
+            return slice(8 + 4 * e, 12 + 4 * e)
         for n in range(4):
             slots("s", n)
+        scan(T.cut[:, :], T.hold[:, :], ps(0, 0, 16), 0.0, A.min, A.add, ["hold", "ps0"], ["cut"])
         slots("c", 0)
         send_codes(0)
-        for d in range(N):
-            ts(T.tt[:, 4 * d:4 * d + 4], T.ii[:, 4 * d:4 * d + 4], ps(4, 128 + d, 129 + d), BIG, A.is_ge, A.mult,
-               ["ii0", "ii1", "ps4"], ["tt%d" % d])
-        tt(meta[:, :], T.ii[:, :], T.tt[:, :], A.add, ["ii0", "ii1", "tt0", "tt1", "tt2", "tt3"], [mk])
-        remote([one(d, meta[:, 4 * d:4 * d + 4], lm[:, place(d)], "arm%d" % t, sp0[d]) for d in oth], [mk])
+        tt(T.flag[:, :], T.ii[:, :], T.cut[:, :], A.is_ge, II + ["cut"], ["flag"])
         slots("c", 1)
+        tt(meta[:, :], T.ii[:, :], T.flag[:, :], A.add, II + ["flag"], [mk])
+        remote([one(d, meta[:, 4 * d:4 * d + 4], lm[:, place(d)], "arm%d" % t, sp0[d]) for d in oth], [mk])
         send_codes(1)
+        slots("c", 2)
         remote([one(e, T[sns][:, 64 * m:64 * m + 64], T[lans][:, me], "ark%d" % t, sp1[e]) for m, e in enumerate(oth)],
                ["%s.%d" % (sns, m) for m in range(3)])
-        slots("c", 2)
         send_codes(2)
         slots("c", 3)
+        if t == 0:
+            quant("eq", "eqs", 0, 512, "et", 0, ["etz"] + ["et%d" % b for b in range(4)], ["eq"])
+            o = [rank] + [s for s in range(N) if s != rank]
+            steps = [-16, 0, 0, 64 * (o[0] - o[1]) + 16, -16, 64 * (o[1] - o[2]) + 16, -16, 64 * (o[2] - o[3]) + 16, -16]
+            fill(T.dd[:, 0:20], -16.0 / 512, "dd")
+            for i, c in enumerate(steps):
+                if c != -16:
+                    run("v", lambda e: e.memset(T.dd[:, i:20:10], c / 512), ["dd"], ["dd%d" % i])
+            for h in range(2):
+                ts(T.dd[:, 10 * h + 9:10 * h + 10], T.qcol[:, :], 64.0 * o[3] + 16 + 32 * h, 1.0 / 512, A.add, A.mult,
+                   ["qcol", "dd"], ["dq%d" % h])
+            fill(T.ab[:, 0:2], FAR, "ab0")
         for b in range(4):
-            mm(4 + b, 128, EQ, 128 * b, CA, 0, ["eq", ca, cas])
+            mm(4 + b, EQ, 128 * b, CA, (0,), ["eq", ca, cas])
         for b in range(4):
-            run("s", lambda e: e.activation(T.hc[:, 32 * b:32 * b + 32], ps(4 + b, G * rank, G * rank + G), AF.Copy, scale=2.0),
-                ["ps%d" % (4 + b)], ["hc%d" % b])
+            act(T.hc[:, 32 * b:32 * b + 32], ps(4 + b, G * rank, G * rank + G), AF.Copy, 0.0, 2.0, ["ps%d" % (4 + b)], ["hc%d" % b])
+        fill(lm[:, 4:8], 8.0, "lp%d" % t)
+        run("v", lambda e: e.tensor_copy(lm[:, 0:4], meta[:, 4 * rank:4 * rank + 4]), [mk], ["lo%d" % t])
         if t == 0:
             late_constants()
-        for h in range(2):
-            tt(T.vv[:, 16 * h:16 * h + 4], meta[:, 4 * rank:4 * rank + 4], T.cv[:, 16 * h:16 * h + 4], A.add,
-               [mk, "cv"], ["vvo%d" % h])
         arrive("arm%d" % t, n_meta, ["lm%d" % t])
+        LM = ["lm%d" % t, "lo%d" % t, "lp%d" % t]
+        DD = ["dd", "dq0", "dq1"] + ["dd%d" % i for i in (1, 2, 3, 5, 7)]
         for h in range(2):
-            tt(T.vv[:, 16 * h + 4:16 * h + 16], lm[:, :], T.cv[:, 16 * h + 4:16 * h + 16], A.add, ["lm%d" % t, "cv"], ["vvr%d" % h])
-        VV = ["vvo0", "vvo1", "vvr0", "vvr1"]
-        run("v", lambda e: e.tensor_tensor_scan(T.pmsc[:, 0:32], T.rsa[:, :], T.vv[:, :], FAR, A.max, A.min), VV + ["rsa"], ["pm"])
-        tt(T.mx[:, 1:32], T.vv[:, 1:32], T.pmsc[:, 0:31], A.max, VV + ["pm"], ["mx"])
-        run("v", lambda e: e.tensor_tensor_scan(T.pmsc[:, 33:64], T.rsb[:, 1:32], T.mx[:, 1:32], FAR, A.max, A.min),
-            ["mx", "rsb"], ["sc"])
+            scan(T.ab[:, 2 + h:22:2], lm[:, h:20:2], T.dd[:, 10 * h:10 * h + 10], FAR, A.min, A.add, LM + DD, ["ab%d" % (1 + h)])
         for h in range(2):
-            c = T.pmsc[:, 47 + 16 * h:48 + 16 * h]
-            ts(T.sz[:, h:h + 1], c, BIG, c, A.is_lt, A.mult, ["sc"], ["sz%d" % h])
-        FS = T.pmsc[:, 15:64:16]
-        ts(T.alst[:, 0:4], FS, 1.0 / 512, None, A.mult, None, ["pm", "sc"], ["alst0"])
+            act(T.junk[:, 10 * h:10 * h + 10], lm[:, h:20:2], AF.Sign, 0.75, -1.0, LM, ["cs%d" % h], T.cs[:, h:h + 1])
+        tt(T.mx[:, 0:20], lm[:, :], T.ab[:, 0:20], A.max, LM + ["ab0", "ab1", "ab2"], ["mx"])
+        F, S = T.ab[:, 20:22], T.sec[:, 9:20:10]
+        ts(T.f5[:, :], F, 512.0, None, A.mult, None, ["ab1", "ab2"], ["f5"])
         for h in range(2):
-            ts(T.alst[:, 4 + h:5 + h], T.sz[:, h:h + 1], T.pmsc[:, 15 + 16 * h:16 + 16 * h], 1.0 / 512, A.max, A.mult,
-               ["sz%d" % h, "pm"], ["alst%d" % (1 + h)])
+            scan(T.sec[:, 10 * h:10 * h + 10], T.mx[:, h:20:2], T.dd[:, 10 * h:10 * h + 10], FAR, A.min, A.add, ["mx"] + DD, ["sc%d" % h])
+        ts(T.alst[:, 2:4], F, 512.0, None, A.mult, None, ["ab1", "ab2"], ["alst1"])
+        ts(T.v2[:, :], T.cs[:, :], -7.0, 512.0, A.is_ge, A.mult, ["cs0", "cs1"], ["v2"])
+        for h in range(2):
+            ts(T.alst[:, h:h + 1], T.sec[:, 10 * h + 9:10 * h + 10], T.v2[:, h:h + 1], T.f5[:, h:h + 1], A.mult, A.max,
+               ["sc%d" % h, "v2", "f5"], ["alst0%d" % h])
 
         def numbers1():
-            run("v", lambda e: e.tensor_copy(T.vi[:, :], FS), ["pm", "sc"], ["vi"])
-            ts(T.val[:, :], FS, BIG, None, A.is_lt, None, ["pm", "sc"], ["val"])
-            ts(T.sv[:, :], T.vi[:, :], 15, None, A.arith_shift_right, None, ["vi"], ["sv"])
-            ts(T.iv[:, :], T.vi[:, :], 511, None, A.bitwise_and, None, ["vi"], ["iv"])
-            ts(T.s192[:, :], T.sv[:, :], float(TOK), 1.0, A.mult, A.add, ["sv"], ["s192"])
+            for i, (k, keys) in enumerate(((F, ["ab1", "ab2"]), (S, ["sc0", "sc1"]))):
+                ts(T.vi[:, 2 * i:2 * i + 2], k, 1.0 / UNIT, None, A.mult, None, keys, ["vi%d" % i])
+                act(T.sg[:, 2 * i:2 * i + 2], k, AF.Sign, 0.75, -1.0, keys, ["sg%d" % i])
+            act(T.wv[:, :], T.sg[:, :], AF.Identity, 2047.5, 2048.5, ["sg0", "sg1"], ["wv"])
+            ts(T.sv[:, :], T.vi[:, :], 15, None, A.arith_shift_right, None, ["vi0", "vi1"], ["sv"])
+            ts(T.iv[:, :], T.vi[:, :], 511, None, A.bitwise_and, None, ["vi0", "vi1"], ["iv"])
 
         def numbers2():
+            ts(T.s192[:, :], T.sv[:, :], float(TOK), None, A.mult, None, ["sv"], ["s192"])
             tt(T.idf[:, :], T.s192[:, :], T.iv[:, :], A.add, ["s192", "iv"], ["idf"])
-            tt(T.idg[:, :], T.idf[:, :], T.val[:, :], A.mult, ["idf", "val"], ["idg"])
+
+        def numbers3():
             for i in range(2):
-                ts(ido[:, i:4:2], T.idg[:, 2 * i:2 * i + 2], -1.0, None, A.add, None, ["idg"], ["ido%d%d" % (t, i)])
+                tt(ido[:, i:4:2], T.idf[:, 2 * i:2 * i + 2], T.wv[:, 2 * i:2 * i + 2], A.min, ["idf", "wv"], ["ido%d%d" % (t, i)])
             for h in range(2):
-                dma("y", T.ids[0:1, 64 * t + 32 * h:64 * t + 32 * h + 32], ido[0:16, 2 * h:2 * h + 2],
+                dma("s" if last and h else "y", T.ids[0:1, 64 * t + 32 * h:64 * t + 32 * h + 32], ido[0:16, 2 * h:2 * h + 2],
                     ["ido%d0" % t, "ido%d1" % t], [], "st")
-        last = t == R - 1
+
+        def outputs():
+            if t == 0:
+                quant("wq", "ws", 0, 128, "wt", 0, ["wt"], ["wq"])
+                quant("ady", "adys", 0, 128, "cbt", 128, ["cbtz"], ["ady", "adys"])
+            pick("c", "ady", 0, 64, land, 0, 640, "alst", 2, AL + [land], ["ady"])
+            pick("s", "adys", 0, 64, lans, 0, 640, "alst", 2, AL + [lans], ["adys"])
+            mm(6, ("wq", "ws"), 0, ("ady", "adys"), (0,), ["wq", "ady", "adys"])
+            for i in range(2):
+                act(yo[:, i:64:2], ps(6, 32 * i, 32 * i + 32), AF.Copy, 0.0, 1.0, ["ps6"], ["yo%d%d" % (t, i)])
+            dma("y", T.y[:, 64 * t:64 * t + 64], yo[:, :], ["yo%d0" % t, "yo%d1" % t], [], "st")
+        ts(T.alst[:, 4:6], S, 512.0, None, A.mult, None, ["sc0", "sc1"], ["alst2"])
         if last:
             numbers1()
         arrive("ark%d" % t, n_tok, [land, lans])
-        AL = ["alst0", "alst1", "alst2", "lz%d" % t]
-        pick("c", "adm", 0, 96, land, 0, 768, "alst", 0, AL + [land], ["adm"])
-        pick("s", "adms", 0, 96, lans, 0, 768, "alst", 0, AL + [lans], ["adms"])
-        for b in range(4):
-            mm(b, 128, EQ, 128 * b, ("adm", "adms"), 0, ["eq", "adm", "adms"])
-        mm(6, 128, ("wq", "ws"), 0, ("adm", "adms"), 0, ["wq", "adm", "adms"])
-        ts(T.mv[:, :], T.pmsc[:, 15:32:16], BIG, float(G * rank - 128), A.is_ge, A.mult, ["pm"], ["mv"])
+        AL = ["alst00", "alst01", "alst1", "alst2", "lz%d" % t]
+        pick("c", "adm", 0, 64, land, 0, 640, "alst", 0, AL + [land], ["adm"])
+        pick("s", "adms", 0, 64, lans, 0, 640, "alst", 0, AL + [lans], ["adms"])
+        for b, ras in ((2, (0,)), (3, (0,)), (0, (0, 32)), (1, (0, 32))):
+            mm(b, EQ, 128 * b, ("adm", "adms"), ras, ["eq", "adm", "adms"])
+        for b in (2, 3):
+            act(T.s4[:, 32 * b:32 * b + 32], ps(b, 32, 64), AF.Copy, 0.0, 1.0, ["ps%d" % b], ["s4%d" % b])
+        ts(T.mv[:, :], F, 1.0, float(G * rank - 128), A.is_ge, A.mult, ["ab1", "ab2"], ["mv"])
+        if last:
+            outputs()
+            numbers2()
         for h in range(2):
             ts(T.clst[:, h:h + 1], T.mv[:, h:h + 1], T.gnew[:, h:h + 1], None, A.add, None, ["mv", "gnew%d" % h], ["clst%d" % h])
         if t == 0:
             await_("v", writers["nt"])
-        for b in range(4):
-            run("s", lambda e: e.activation(T.s4[:, 32 * b:32 * b + 32], ps(b, 64, 96), AF.Copy), ["ps%d" % b], ["s4%d" % b])
-        for i in range(2):
-            run("s", lambda e: e.activation(yo[:, i:64:2], ps(6, 32 * i, 32 * i + 32), AF.Copy), ["ps6"], ["yo%d%d" % (t, i)])
-        if last:
-            numbers2()
-        dma("y", T.y[:, 64 * t:64 * t + 64], yo[:, :], ["yo%d0" % t, "yo%d1" % t], [], "st")
-        for b in range(5):
-            if b < 4:
-                tt(T.hh[:, 32 * b:32 * b + 32], ps(b, 0, 32), T.s4[:, 32 * b:32 * b + 32], A.add, ["ps%d" % b, "s4%d" % b], ["hh%d" % b])
-            if b > 0:
-                a = b - 1
-                tt(T.nt[:, a:128:4], T.hh[:, 32 * a:32 * a + 32], T.hc[:, 32 * a:32 * a + 32], A.add, ["hh%d" % a, "hc%d" % a], ["nt%d" % a])
+
+        def half(b, part, key):
+            tt(T.nt[:, b:128:4], part, T.hc[:, 32 * b:32 * b + 32], A.add, [key, "hc%d" % b], ["nt%d" % b])
+        for b in (2, 3):
+            tt(T.hh[:, 32 * b:32 * b + 32], ps(b, 0, 32), T.s4[:, 32 * b:32 * b + 32], A.add, ["ps%d" % b, "s4%d" % b], ["hh%d" % b])
+        half(0, ps(0, 0, 32), "ps0")
+        half(2, T.hh[:, 64:96], "hh2")
+        half(3, T.hh[:, 96:128], "hh3")
+        half(1, ps(1, 0, 32), "ps1")
         run("v", lambda e: e.quantize_mx(T[ca][:, 128:256], T[cas][:, 128:256], T.nt[:, :]), ["nt", "nt0", "nt1", "nt2", "nt3"], [ca + "n"])
         cn, cns = "ca%d" % (t + 1), "cas%d" % (t + 1)
         CL = ["clst0", "clst1", ca + "n"]
@@ -462,15 +480,21 @@ def rank_program(g, core, T, topo):
         if last:
             dma("y", T.oc[:, :], T[cn][:, own].bitcast(dt.uint8), [cn], [], "st")
             for k in range(4):
-                dma("y" if k % 2 else "s", T.osc[4 * k:4 * k + 4, :], T[cns][32 * k:32 * k + 4, own], [cns], [], "st")
+                dma("y" if k == 3 else "s", T.osc[4 * k:4 * k + 4, :], T[cns][32 * k:32 * k + 4, own], [cns], [], "st")
+            numbers3()
         else:
             remote([many(T[cn][:, own].bitcast(dt.uint8), T[cn][:, own].bitcast(dt.uint8), "arc%d" % (t + 1))], [cn])
             remote([many(T[cns][:, own], T[cns][:, own], "arc%d" % (t + 1))], [cns])
             quant("xq", "xs", 192 * t + 192, 192 * t + 384, "xt", 768 * t + 768, ["xt%d" % (t + 1)], ["xq%d" % (t + 1)])
+            outputs()
             numbers1()
+            zero_block(t + 1)
             numbers2()
-            quant("land%d" % (t + 1), "lans%d" % (t + 1), 512, 768, "zt", 0, ["zt0", "zt1"], ["lz%d" % (t + 1)])
+            numbers3()
             arrive("arc%d" % (t + 1), n_cen, [cn, cns])
+            if t == 0:
+                await_("y", writers["ca1"])
+                dma("y", T.xt[:, 1536:2304], T.x[:, 1536:2304], [], ["xt2"], "ldx2")
     for k in cnt:
         if know["p"].get(k, 0) < cnt[k]:
             g.wait_ge(T.sem[k], cnt[k])

from concourse.bass import DstId, RemoteDMATransfer
from concourse.mybir import dt, AluOpType as A, ActivationFunctionType as AF

CODE = "float8_e4m3fn_x4"
N, G, TOK, R, CAPP = 4, 32, 192, 3, 64
UNIT = 2.0 ** -18
WIN = 512
FAR = 64.0
LOW = -1.0e29
LIFT = 1024.0

SCRATCH = {
    "cbt": ("sbuf", [128, 768], "bfloat16"), "xt": ("sbuf", [128, 2304], "bfloat16"), "wt": ("sbuf", [128, 512], "bfloat16"),
    "pt": ("sbuf", [128, 512], "bfloat16"), "zz": ("sbuf", [128, 512], "bfloat16"),
    "ptx": ("sbuf", [128, 512], "bfloat16"), "zzx": ("sbuf", [128, 512], "bfloat16"),
    "nt": ("sbuf", [128, 512], "bfloat16"), "ct": ("sbuf", [128, 2048], "bfloat16"), "et": ("sbuf", [128, 2048], "bfloat16"),
    "idf": ("sbuf", [128, 4], "float32"), "ps": ("psum", [128, 4096], "float32"),
}
for _c, _s, _n in (("cq", "cqs", 512), ("eq", "eqs", 512), ("cbq", "cbs", 128), ("xq", "xs", 576), ("wq", "ws", 128),
                   ("pq", "pqs", 128), ("zq", "zqs", 128), ("pxq", "pxs", 128), ("zxq", "zxs", 128), ("adm", "adms", 160),
                   ("ady", "adys", 128)):
    SCRATCH[_c] = ("sbuf", [128, _n], CODE)
    SCRATCH[_s] = ("sbuf", [128, _n], "uint8")
for _b in ("rowi", "k16", "negc", "ma", "mb", "msk", "ls1", "ls2", "dist", "hc", "s4", "hh"):
    SCRATCH[_b] = ("sbuf", [128, 128], "float32")
for _b in ("pcol", "npcol", "qcol", "corr", "ncorr"):
    SCRATCH[_b] = ("sbuf", [128, 1], "float32")
for _b in ("dd", "ab", "mx", "sec", "junk"):
    SCRATCH[_b] = ("sbuf", [128, 32], "float32")
for _b, _n, _d in (("pi", 1, "int32"), ("qi", 1, "int32"), ("ii", 16, "float32"), ("hold", 16, "float32"), ("cut", 16, "float32"),
                   ("flag", 16, "float32"), ("lst", 16, "uint16"), ("cs", 2, "float32"), ("v2", 2, "float32"),
                   ("f5", 2, "float32"), ("alst", 6, "uint16"), ("mv", 2, "float32"), ("clst", 2, "uint16"),
                   ("ilst", 2, "uint16"), ("gnew", 2, "float32"), ("vi", 4, "int32"), ("iv", 4, "int32"), ("sv", 4, "int32"),
                   ("s192", 4, "float32"), ("sg", 4, "float32"), ("wv", 4, "float32")):
    SCRATCH[_b] = ("sbuf", [128, _n], _d)
for _t in range(R):
    SCRATCH["meta%d" % _t] = ("sbuf", [128, 16], "bfloat16")
    SCRATCH["lm%d" % _t] = ("sbuf", [128, 20], "bfloat16")
    SCRATCH["snd%d" % _t] = ("sbuf", [128, 192], CODE)
    SCRATCH["sns%d" % _t] = ("sbuf", [128, 192], "uint8")
    SCRATCH["land%d" % _t] = ("sbuf", [128, 640], CODE)
    SCRATCH["lans%d" % _t] = ("sbuf", [128, 640], "uint8")
    SCRATCH["yo%d" % _t] = ("sbuf", [128, 64], "float32")
    SCRATCH["ido%d" % _t] = ("sbuf", [128, 4], "float32")
for _t in range(R + 1):
    SCRATCH["ca%d" % _t] = ("sbuf", [128, 256], CODE)
    SCRATCH["cas%d" % _t] = ("sbuf", [128, 256], "uint8")
SEMAPHORES = ["qv", "qs", "qt", "qp", "ldcb", "ldx0", "ldx1", "ldx2", "ldw", "st", "sent",
              "arc0", "arc1", "arc2", "arm0", "arm1", "arm2", "ark0", "ark1", "ark2"]


def rank_program(g, core, T, topo):
    rank = T.rank_of(core)
    if rank is None:
        return
    cores = list(T.cores)

    def others(r):
        def hops(d):
            a, b = topo.chip(cores[r]), topo.chip(cores[d])
            return 0 if a == b else (1 if topo.mates(a, b) or topo.same_plane(a, b) else 2)
        return sorted([d for d in range(N) if d != r], key=lambda d: -hops(d))

    def bits(es):
        m = 0
        for e in es:
            m |= 1 << e
        return m

    def common(r):
        es = topo.engines(cores[r], cores[others(r)[0]])
        for d in others(r):
            es = [e for e in es if e in topo.engines(cores[r], cores[d])]
        return es

    def split(r, kind):
        es = common(r)
        h, q = len(es) // 2, len(es) // 4
        a, b, c = others(r)
        if kind == 0:
            return {a: es[:h], b: es[h:h + q], c: es[h + q:]}
        return {a: es[h:], b: es[:q], c: es[q:h]}

    oth = others(rank)
    full = common(rank)
    dst = {}
    for d in oth:
        rid, pid, _ = topo.addr(cores[d])
        dst[d] = (rid, pid)
    n_meta = sum(len(split(s, 0)[rank]) for s in range(N) if s != rank)
    n_tok = sum(len(split(s, 1)[rank]) + len(common(s)) for s in range(N) if s != rank)
    n_cen = sum(2 * len(common(s)) for s in range(N) if s != rank)

    ENG = {"v": g.vector, "s": g.scalar, "t": g.tensor, "p": g, "y": g.sync}
    cnt = {}
    know = {q: {} for q in ENG}
    writers, readers = {}, {}

    def await_(q, recs):
        recs = [r for r in recs if know[q].get(r[0], 0) < r[1]]
        keep = []
        for i, r in enumerate(recs):
            if any(o is not r and o[2].get(r[0], 0) >= r[1] and not (o[0] == r[0] and o[1] == r[1] and j > i)
                   for j, o in enumerate(recs)):
                continue
            keep.append(r)
        for r in keep:
            if know[q].get(r[0], 0) < r[1]:
                ENG[q].wait_ge(T.sem[r[0]], r[1])
            for k, v in r[2].items():
                know[q][k] = max(know[q].get(k, 0), v)
        for r in recs:
            for k, v in r[2].items():
                know[q][k] = max(know[q].get(k, 0), v)

    def deps(q, rd, wr):
        recs = []
        for k in rd:
            recs += [r for r in writers.get(k, [])]
            if k[:2] == "ps":
                recs += [r for r in readers.get(k, []) if r[3] != q]
        for k in wr:
            recs += writers.get(k, []) + readers.get(k, [])
        return recs

    def note(rec, rd, wr):
        for k in wr:
            writers[k], readers[k] = [rec], []
        for k in rd:
            if k not in wr:
                readers.setdefault(k, []).append(rec)

    def record(q, sem, n):
        cnt[sem] = cnt.get(sem, 0) + n
        clk = dict(know[q])
        clk[sem] = cnt[sem]
        return (sem, cnt[sem], clk, q)

    def run(q, f, rd, wr):
        await_(q, deps(q, rd, wr))
        f(ENG[q]).then_inc(T.sem["q" + q], 1)
        note(record(q, "q" + q, 1), rd, wr)

    def dma(q, out, in_, rd, wr, sem):
        await_(q, deps(q, rd, wr))
        ENG[q].dma_start(out, in_).then_inc(T.sem[sem], 16)
        note(record(q, sem, 16), rd, wr)

    def arrive(sem, n, keys):
        cnt[sem] = n
        rec = (sem, n, {sem: n}, "r")
        for k in keys:
            writers.setdefault(k, []).append(rec)

    def remote(transfers, rd):
        await_("p", deps("p", rd, []))
        g.remote_dma_fused([t for t, _ in transfers], local_sem=T.sem["sent"])
        cnt["sent"] = cnt.get("sent", 0) + sum(n for _, n in transfers)

    def one(d, src, to, sem, es):
        return (RemoteDMATransfer(dst_ids=[DstId(rid=dst[d][0], pnc=dst[d][1])], dma_engine_mask=bits(es),
                                  remote_sem=T.sem[sem], src=src, dst=to), len(es))

    def many(src, to, sem):
        return (RemoteDMATransfer(dst_ids=[DstId(rid=dst[d][0], pnc=dst[d][1]) for d in oth], dma_engine_mask=bits(full),
                                  remote_sem=T.sem[sem], srcs=[src], dsts=[to for d in oth]), len(full))

    def ts(out, in0, s1, s2, o0, o1, rd, wr):
        if o1 is None:
            run("v", lambda e: e.tensor_scalar(out, in0, s1, None, o0), rd, wr)
        else:
            run("v", lambda e: e.tensor_scalar(out, in0, s1, s2, o0, o1), rd, wr)

    def tt(out, a, b, op, rd, wr):
        run("v", lambda e: e.tensor_tensor(out, a, b, op), rd, wr)

    def scan(out, a, b, first, o0, o1, rd, wr):
        run("v", lambda e: e.tensor_tensor_scan(out, a, b, first, o0, o1), rd, wr)

    def act(out, in_, func, bias, scale, rd, wr, total=None):
        run("s", lambda e: e.activation(out, in_, func, bias=bias, scale=scale, accum_out=total), rd, wr)

    def fill(ap, c, key):
        run("v", lambda e: e.memset(ap, c), [], [key])

    def flat(out, in_, c, rd, key):
        act(out, in_, AF.Identity, c, 0.0, rd, [key])

    def quant(c, s, a, b, tile, x, keys, out):
        run("v", lambda e: e.quantize_mx(T[c][:, a:b], T[s][:, a:b], T[tile][:, x:x + 4 * (b - a)]), keys, out)

    def mm(bank, l, la, r, ras, rd):
        lc, lsc = l
        rc, rs = r
        await_("t", deps("t", rd, ["ps%d" % bank]))
        for i, ra in enumerate(ras):
            call = g.tensor.matmul_mx(T.ps[:, 512 * bank:512 * bank + 128], T[lc][:, la:la + 128], T[lsc][:, la:la + 128],
                                      T[rc][:, ra:ra + 128], T[rs][:, ra:ra + 128], i == 0, i == len(ras) - 1)
        call.then_inc(T.sem["qt"], 1)
        note(record("t", "qt", 1), rd, ["ps%d" % bank])

    def pick(kind, dstb, da, n, srcb, sa, sb, lstb, la, rd, wr):
        k = n // 16
        if kind == "c":
            run("v", lambda e: e.tensor_copy(T[dstb][:, da:da + n].bitcast(dt.uint32),
                                             T[srcb][:, sa:sb].bitcast(dt.uint32).indirect(T[lstb][:, la:la + k])), rd, wr)
        else:
            run("s", lambda e: e.activation(T[dstb][:, da:da + n],
                                            T[srcb][:, sa:sb].indirect(T[lstb][:, la:la + k]), AF.Copy), rd, wr)

    def iota(out, pattern, base, mult, key, imprecise=True):
        if imprecise:
            run("p", lambda e: e.iota(out, pattern, base, mult, allow_small_or_imprecise_dtypes=True), [], [key])
        else:
            run("p", lambda e: e.iota(out, pattern, base, mult), [], [key])

    def ps(bank, a, b, p0=0):
        return T.ps[p0:128, 512 * bank + a:512 * bank + b]

    dma("y", T.cbt[:, 0:128], T.cb[:, :], [], ["cbt"], "ldcb")
    dma("y", T.xt[:, 0:768], T.x[:, 0:768], [], ["xt0"], "ldx0")

    iota(T.pi[:, :], [[1, 1]], 0, 1, "pi", False)
    iota(T.rowi[:, :], [[1, 128]], 0, 0, "rowi")
    iota(T.pcol[:, :], [[1, 1]], 0, 1, "pcol")
    iota(T.npcol[:, :], [[1, 1]], 0, -1, "npcol")
    iota(T.k16[:, :], [[0, 8], [1, 16]], 0, 0, "k16")
    fill(T.et[:, :], 0.0, "etz")
    fill(T.cbt[:, 128:768], 0.0, "cbtz")
    ts(T.qi[:, :], T.pi[:, :], 15, None, A.bitwise_and, None, ["pi"], ["qi"])
    run("v", lambda e: e.tensor_copy(T.qcol[:, :], T.qi[:, :]), ["qi"], ["qcol"])
    for h in range(2):
        ts(T.ilst[:, h:h + 1], T.qcol[:, :], 16.0 * h, None, A.add, None, ["qcol"], ["ilst%d" % h])
    for key, sl, c in (("ct0c", slice(1, 512, 4), 0.0), ("ct0d", slice(3, 512, 4), 0.0), ("ct1a", slice(512, 1024, 4), 1.0),
                       ("ct1b", slice(514, 1024, 4), -1.0)):
        flat(T.ct[:, sl], T.rowi[:, :], c, ["rowi"], key)

    quant("cbq", "cbs", 0, 128, "cbt", 0, ["cbt", "cbtz"], ["cbq"])
    own = slice(G * rank, G * rank + G)
    remote([many(T.cbq[:, 0:G].bitcast(dt.uint8), T.ca0[:, own].bitcast(dt.uint8), "arc0")], ["cbq"])
    remote([many(T.cbs[:, 0:G], T.cas0[:, own], "arc0")], ["cbq"])
    pick("c", "ca0", G * rank, G, "cbq", 0, 128, "ilst", 0, ["cbq", "ilst0", "ilst1"], ["ca0"])
    pick("s", "cas0", G * rank, G, "cbs", 0, 128, "ilst", 0, ["cbq", "ilst0", "ilst1"], ["cas0"])
    arrive("arc0", n_cen, ["ca0", "cas0"])
    iota(T.ptx[:, :], [[0, 512]], 0, 0, "ptx")
    iota(T.zzx[:, :], [[0, 512]], 0, 0, "zzx")
    iota(T.hold[:, :], [[0, 4], [1, 4]], 0, 0, "hold")
    for i, c in enumerate((1.0, 1.0, 0.0, 0.0)):
        flat(T.ct[:, 1024 + i:1536:4], T.rowi[:, :], c, ["rowi"], "ct2%d" % i)
    fill(T.negc[:, :], LOW, "negc")
    ts(T.ct[:, 0:512:4], T.rowi[:, :], T.pcol[:, :], None, A.is_ge, None, ["rowi", "pcol"], ["ct0a"])
    ts(T.ct[:, 2:512:4], T.rowi[:, :], T.pcol[:, :], -1.0, A.is_ge, A.mult, ["rowi", "pcol"], ["ct0b"])
    for i, c in enumerate((0.0, -1.0, 1.0, 1.0)):
        fill(T.ct[:, 1536 + i:2048:4], c, "ct3%d" % i)
    ts(T.ct[64:128, 513:1024:4], T.rowi[64:128, :], T.pcol[64:128, :], None, A.is_ge, None, ["rowi", "pcol"], ["ct1c"])
    ts(T.ct[64:128, 515:1024:4], T.rowi[64:128, :], T.pcol[64:128, :], -1.0, A.is_ge, A.mult, ["rowi", "pcol"], ["ct1d"])
    fill(T.ct[0:64, 513:1024:4], 0.0, "ct1e")
    fill(T.ct[0:64, 515:1024:4], 0.0, "ct1f")
    fill(T.pt[:, :], 0.0, "pt")
    fill(T.zz[0:64, 1:512:4], 0.0, "zza")
    fill(T.zz[0:64, 3:512:4], 0.0, "zzb")
    fill(T.pt[:, 0:1], 1.0, "pt")
    fill(T.pt[64:128, 1:2], 1.0, "pt")
    quant("cq", "cqs", 0, 512, "ct", 0, ["ct0a", "ct0b", "ct0c", "ct0d", "ct1a", "ct1b", "ct1c", "ct1d", "ct1e", "ct1f"]
          + ["ct%d%d" % (b, i) for b in (2, 3) for i in range(4)], ["cq"])
    ts(T.msk[:, :], T.k16[:, :], T.qcol[:, :], -33.0 * LIFT, A.is_equal, A.mult, ["k16", "qcol"], ["msk"])
    ts(T.corr[:, :], T.qcol[:, :], -LIFT, 15.0 * LIFT, A.mult, A.add, ["qcol"], ["corr"])
    quant("xq", "xs", 0, 192, "xt", 0, ["xt0"], ["xq0"])
    ts(T.msk[:, :], T.msk[:, :], LIFT, None, A.add, None, [], ["msk"])
    ts(T.ncorr[:, :], T.corr[:, :], -UNIT, None, A.mult, None, ["corr"], ["ncorr"])
    fill(T.ptx[:, 0:1], 1.0, "ptx")
    fill(T.ptx[64:128, 1:2], 1.0, "ptx")
    act(T.dist[:, :], T.rowi[:, :], AF.Abs, T.npcol[:, 0:1], 1.0, ["rowi", "npcol"], ["dist"])
    for b in range(4):
        act(T.et[:, 512 * b + b:512 * b + 512:4], T.dist[:, :], AF.Relu, 0.25, -0.25, ["dist", "etz"], ["et%d" % b])
    await_("y", writers["ca0"])
    dma("y", T.wt[:, :], T.w[:, :], [], ["wt"], "ldw")
    dma("y", T.xt[:, 768:1536], T.x[:, 768:1536], [], ["xt1"], "ldx1")

    def zero_block(t):
        quant("land%d" % t, "lans%d" % t, WIN, WIN + 128, "cbt", 128, ["cbtz"], ["lz%d" % t])

    def late_constants():
        flat(T.nt[:, :], T.cbt[:, 128:640], 0.0, ["cbtz"], "nt")
        for h in range(2):
            ts(T.gnew[:, h:h + 1], T.qcol[:, :], 128.0 + 16 * h, None, A.add, None, ["qcol"], ["gnew%d" % h])
        quant("adm", "adms", 0, 160, "cbt", 128, ["cbtz"], ["adm", "adms"])
        zero_block(0)

    XQ, CQ, EQ = ("xq", "xs"), ("cq", "cqs"), ("eq", "eqs")
    for t in range(R):
        last = t == R - 1
        ca, cas = "ca%d" % t, "cas%d" % t
        CA = (ca, cas)
        lm, meta, yo, ido = T["lm%d" % t], T["meta%d" % t], T["yo%d" % t], T["ido%d" % t]
        land, lans, snd, sns = "land%d" % t, "lans%d" % t, "snd%d" % t, "sns%d" % t
        mm(0, XQ, 192 * t, CA, (0,), ["xq%d" % t, ca, cas])
        mm(1, XQ, 192 * t + 64, CA, (0,), ["xq%d" % t, ca, cas])
        scan(T.ma[:, :], ps(0, 0, 128), T.negc[:, :], LOW, A.max, A.max, ["ps0", "negc"], ["ma"])
        scan(T.mb[64:128, :], ps(1, 0, 128, 64), T.negc[64:128, :], LOW, A.max, A.max, ["ps1", "negc"], ["mb"])

        def before(q, out, m, key, p0, k0, k1, step, wr):
            if q == "v":
                ts(out, m[p0:128, k0:k1:step], m[p0:128, 127:128], None, A.is_lt, None, [key], [wr])
            else:
                act(out, m[p0:128, k0:k1:step], AF.Sign, m[p0:128, 127:128], -1.0, [key], [wr])
        if t == 0:
            await_("s", writers["pt"] + writers["ptx"])
            await_("v", writers["pt"] + writers["ptx"])
        before("s", T.pt[:, 4:512:4], T.ma, "ma", 0, 0, 127, 1, "pt0")
        before("s", T.pt[:, 2:512:4], T.ma, "ma", 0, 0, 128, 1, "pt2")
        before("v", T.pt[64:128, 5:512:4], T.mb, "mb", 64, 0, 127, 1, "pt1")
        before("v", T.pt[64:128, 3:512:4], T.mb, "mb", 64, 0, 128, 1, "pt3")
        before("v", T.ptx[64:128, 5:14:4], T.mb, "mb", 64, 31, 96, 32, "px1")
        before("v", T.ptx[64:128, 3:12:4], T.mb, "mb", 64, 31, 96, 32, "px3")
        quant("pq", "pqs", 0, 128, "pt", 0, ["pt", "pt0", "pt1", "pt2", "pt3"], ["pq"])
        before("s", T.ptx[:, 4:13:4], T.ma, "ma", 0, 31, 96, 32, "px0")
        before("s", T.ptx[:, 2:11:4], T.ma, "ma", 0, 31, 96, 32, "px2")
        mm(3, CQ, 128, ("pq", "pqs"), (0,), ["cq", "pq"])
        mm(2, CQ, 0, ("pq", "pqs"), (0,), ["cq", "pq"])
        quant("pxq", "pxs", 0, 128, "ptx", 0, ["ptx", "px0", "px1", "px2", "px3"], ["pxq"])
        mm(6, CQ, 0, ("pxq", "pxs"), (0,), ["cq", "pxq"])
        mm(7, CQ, 128, ("pxq", "pxs"), (0,), ["cq", "pxq"])
        for el, c in ((1, 1.0), (3, 2.0)):
            act(T.zz[64:128, el:512:4], ps(3, 0, 128, 64), AF.Relu, c, -1.0, ["ps3"], ["zz%d" % el])
        for el, c in ((0, 1.0), (2, 2.0)):
            ts(T.zz[:, el:512:4], ps(2, 0, 128), c, None, A.is_lt, None, ["ps2"], ["zz%d" % el])
        quant("zq", "zqs", 0, 128, "zz", 0, ["zza", "zzb", "zz0", "zz1", "zz2", "zz3"], ["zq"])
        mm(4, CQ, 256, ("zq", "zqs"), (0,), ["cq", "zq"])
        mm(5, CQ, 384, ("zq", "zqs"), (0,), ["cq", "zq"])
        for el, bank, p0 in ((0, 6, 0), (1, 7, 64)):
            ts(T.zzx[p0:128, el:64:16], ps(bank, 0, 4, p0), CAPP + 1.0, UNIT, A.is_lt, A.mult, ["ps%d" % bank, "zzx"], ["zx%d" % el])
        quant("zxq", "zxs", 0, 128, "zzx", 0, ["zzx", "zx0", "zx1"], ["zxq"])
        mm(0, CQ, 256, ("zxq", "zxs"), (0,), ["cq", "zxq"])
        for j, ls in ((0, T.ls1), (1, T.ls2)):
            scan(ls[:, :], T.msk[:, :], ps(4 + j, 0, 128), 0.0, A.add, A.max, ["ps%d" % (4 + j), "msk"], ["ls%d" % j])
        for j, ls in ((0, T.ls1), (1, T.ls2)):
            for h in range(2):
                act(T.ii[:, 2 * j + h:16:4], ls[:, 15 + 16 * h:128:32], AF.Identity, T.ncorr[:, 0:1], UNIT, ["ls%d" % j, "ncorr"],
                    ["ii%d%d" % (j, h)])
            ts(T.lst[:, j:16:2], ls[:, 15:128:16], T.corr[:, 0:1], float(TOK - 1), A.subtract, A.min,
               ["ls%d" % j, "corr"], ["lst%d" % j])
        II = ["ii00", "ii01", "ii10", "ii11"]
        LST = ["lst0", "lst1"]
        mk = "meta%d" % t
        sp0, sp1 = split(rank, 0), split(rank, 1)
        me = slice(64 * rank, 64 * rank + 64)

        def slots(kind, n):
            d = (oth + [rank])[n]
            b, x = (snd, "xq") if kind == "c" else (sns, "xs")
            o = land if kind == "c" else lans
            if n < 3:
                pick(kind, b, 64 * n, 64, x, 192 * t, 192 * t + 192, "lst", 4 * d, LST + ["xq%d" % t], ["%s.%d" % (b, n)])
            else:
                pick(kind, o, 64 * rank, 64, x, 192 * t, 192 * t + 192, "lst", 4 * d, LST + ["xq%d" % t], [o])

        def send_codes(n):
            remote([one(oth[n], T[snd][:, 64 * n:64 * n + 64].bitcast(dt.uint8), T[land][:, me].bitcast(dt.uint8), "ark%d" % t, full)],
                   ["%s.%d" % (snd, n)])

        def place(d):
            e = [s for s in range(N) if s != d].index(rank)
            return slice(8 + 4 * e, 12 + 4 * e)
        for n in range(4):
            slots("s", n)
        scan(T.cut[:, :], T.hold[:, :], ps(0, 0, 16), 0.0, A.min, A.add, ["hold", "ps0"], ["cut"])
        slots("c", 0)
        send_codes(0)
        tt(T.flag[:, :], T.ii[:, :], T.cut[:, :], A.is_ge, II + ["cut"], ["flag"])
        slots("c", 1)
        tt(meta[:, :], T.ii[:, :], T.flag[:, :], A.add, II + ["flag"], [mk])
        remote([one(d, meta[:, 4 * d:4 * d + 4], lm[:, place(d)], "arm%d" % t, sp0[d]) for d in oth], [mk])
        send_codes(1)
        slots("c", 2)
        remote([one(e, T[sns][:, 64 * m:64 * m + 64], T[lans][:, me], "ark%d" % t, sp1[e]) for m, e in enumerate(oth)],
               ["%s.%d" % (sns, m) for m in range(3)])
        send_codes(2)
        slots("c", 3)
        if t == 0:
            quant("eq", "eqs", 0, 512, "et", 0, ["etz"] + ["et%d" % b for b in range(4)], ["eq"])
            o = [rank] + [s for s in range(N) if s != rank]
            steps = [-16, 0, 0, 64 * (o[0] - o[1]) + 16, -16, 64 * (o[1] - o[2]) + 16, -16, 64 * (o[2] - o[3]) + 16, -16]
            fill(T.dd[:, 0:20], -16.0 / 512, "dd")
            for i, c in enumerate(steps):
                if c != -16:
                    run("v", lambda e: e.memset(T.dd[:, i:20:10], c / 512), ["dd"], ["dd%d" % i])
            for h in range(2):
                ts(T.dd[:, 10 * h + 9:10 * h + 10], T.qcol[:, :], 64.0 * o[3] + 16 + 32 * h, 1.0 / 512, A.add, A.mult,
                   ["qcol", "dd"], ["dq%d" % h])
            fill(T.ab[:, 0:2], FAR, "ab0")
        for b in range(4):
            mm(4 + b, EQ, 128 * b, CA, (0,), ["eq", ca, cas])
        for b in range(4):
            act(T.hc[:, 32 * b:32 * b + 32], ps(4 + b, G * rank, G * rank + G), AF.Copy, 0.0, 2.0, ["ps%d" % (4 + b)], ["hc%d" % b])
        fill(lm[:, 4:8], 8.0, "lp%d" % t)
        run("v", lambda e: e.tensor_copy(lm[:, 0:4], meta[:, 4 * rank:4 * rank + 4]), [mk], ["lo%d" % t])
        if t == 0:
            late_constants()
        arrive("arm%d" % t, n_meta, ["lm%d" % t])
        LM = ["lm%d" % t, "lo%d" % t, "lp%d" % t]
        DD = ["dd", "dq0", "dq1"] + ["dd%d" % i for i in (1, 2, 3, 5, 7)]
        for h in range(2):
            scan(T.ab[:, 2 + h:22:2], lm[:, h:20:2], T.dd[:, 10 * h:10 * h + 10], FAR, A.min, A.add, LM + DD, ["ab%d" % (1 + h)])
        for h in range(2):
            act(T.junk[:, 10 * h:10 * h + 10], lm[:, h:20:2], AF.Sign, 0.75, -1.0, LM, ["cs%d" % h], T.cs[:, h:h + 1])
        tt(T.mx[:, 0:20], lm[:, :], T.ab[:, 0:20], A.max, LM + ["ab0", "ab1", "ab2"], ["mx"])
        F, S = T.ab[:, 20:22], T.sec[:, 9:20:10]
        ts(T.f5[:, :], F, 512.0, None, A.mult, None, ["ab1", "ab2"], ["f5"])
        for h in range(2):
            scan(T.sec[:, 10 * h:10 * h + 10], T.mx[:, h:20:2], T.dd[:, 10 * h:10 * h + 10], FAR, A.min, A.add, ["mx"] + DD, ["sc%d" % h])
        ts(T.alst[:, 2:4], F, 512.0, None, A.mult, None, ["ab1", "ab2"], ["alst1"])
        ts(T.v2[:, :], T.cs[:, :], -7.0, 512.0, A.is_ge, A.mult, ["cs0", "cs1"], ["v2"])
        for h in range(2):
            ts(T.alst[:, h:h + 1], T.sec[:, 10 * h + 9:10 * h + 10], T.v2[:, h:h + 1], T.f5[:, h:h + 1], A.mult, A.max,
               ["sc%d" % h, "v2", "f5"], ["alst0%d" % h])

        def numbers1():
            for i, (k, keys) in enumerate(((F, ["ab1", "ab2"]), (S, ["sc0", "sc1"]))):
                ts(T.vi[:, 2 * i:2 * i + 2], k, 1.0 / UNIT, None, A.mult, None, keys, ["vi%d" % i])
                act(T.sg[:, 2 * i:2 * i + 2], k, AF.Sign, 0.75, -1.0, keys, ["sg%d" % i])
            act(T.wv[:, :], T.sg[:, :], AF.Identity, 2047.5, 2048.5, ["sg0", "sg1"], ["wv"])
            ts(T.sv[:, :], T.vi[:, :], 15, None, A.arith_shift_right, None, ["vi0", "vi1"], ["sv"])
            ts(T.iv[:, :], T.vi[:, :], 511, None, A.bitwise_and, None, ["vi0", "vi1"], ["iv"])

        def numbers2():
            ts(T.s192[:, :], T.sv[:, :], float(TOK), None, A.mult, None, ["sv"], ["s192"])
            tt(T.idf[:, :], T.s192[:, :], T.iv[:, :], A.add, ["s192", "iv"], ["idf"])

        def numbers3():
            for i in range(2):
                tt(ido[:, i:4:2], T.idf[:, 2 * i:2 * i + 2], T.wv[:, 2 * i:2 * i + 2], A.min, ["idf", "wv"], ["ido%d%d" % (t, i)])
            for h in range(2):
                dma("s" if last and h else "y", T.ids[0:1, 64 * t + 32 * h:64 * t + 32 * h + 32], ido[0:16, 2 * h:2 * h + 2],
                    ["ido%d0" % t, "ido%d1" % t], [], "st")

        def outputs():
            if t == 0:
                quant("wq", "ws", 0, 128, "wt", 0, ["wt"], ["wq"])
                quant("ady", "adys", 0, 128, "cbt", 128, ["cbtz"], ["ady", "adys"])
            pick("c", "ady", 0, 64, land, 0, 640, "alst", 2, AL + [land], ["ady"])
            pick("s", "adys", 0, 64, lans, 0, 640, "alst", 2, AL + [lans], ["adys"])
            mm(6, ("wq", "ws"), 0, ("ady", "adys"), (0,), ["wq", "ady", "adys"])
            for i in range(2):
                act(yo[:, i:64:2], ps(6, 32 * i, 32 * i + 32), AF.Copy, 0.0, 1.0, ["ps6"], ["yo%d%d" % (t, i)])
            dma("y", T.y[:, 64 * t:64 * t + 64], yo[:, :], ["yo%d0" % t, "yo%d1" % t], [], "st")
        ts(T.alst[:, 4:6], S, 512.0, None, A.mult, None, ["sc0", "sc1"], ["alst2"])
        if last:
            numbers1()
        arrive("ark%d" % t, n_tok, [land, lans])
        AL = ["alst00", "alst01", "alst1", "alst2", "lz%d" % t]
        pick("c", "adm", 0, 64, land, 0, 640, "alst", 0, AL + [land], ["adm"])
        pick("s", "adms", 0, 64, lans, 0, 640, "alst", 0, AL + [lans], ["adms"])
        for b, ras in ((2, (0,)), (3, (0,)), (0, (0, 32)), (1, (0, 32))):
            mm(b, EQ, 128 * b, ("adm", "adms"), ras, ["eq", "adm", "adms"])
        for b in (2, 3):
            act(T.s4[:, 32 * b:32 * b + 32], ps(b, 32, 64), AF.Copy, 0.0, 1.0, ["ps%d" % b], ["s4%d" % b])
        ts(T.mv[:, :], F, 1.0, float(G * rank - 128), A.is_ge, A.mult, ["ab1", "ab2"], ["mv"])
        if last:
            outputs()
            numbers2()
        for h in range(2):
            ts(T.clst[:, h:h + 1], T.mv[:, h:h + 1], T.gnew[:, h:h + 1], None, A.add, None, ["mv", "gnew%d" % h], ["clst%d" % h])
        if t == 0:
            await_("v", writers["nt"])

        def half(b, part, key):
            tt(T.nt[:, b:128:4], part, T.hc[:, 32 * b:32 * b + 32], A.add, [key, "hc%d" % b], ["nt%d" % b])
        for b in (2, 3):
            tt(T.hh[:, 32 * b:32 * b + 32], ps(b, 0, 32), T.s4[:, 32 * b:32 * b + 32], A.add, ["ps%d" % b, "s4%d" % b], ["hh%d" % b])
        half(0, ps(0, 0, 32), "ps0")
        half(2, T.hh[:, 64:96], "hh2")
        half(3, T.hh[:, 96:128], "hh3")
        half(1, ps(1, 0, 32), "ps1")
        run("v", lambda e: e.quantize_mx(T[ca][:, 128:256], T[cas][:, 128:256], T.nt[:, :]), ["nt", "nt0", "nt1", "nt2", "nt3"], [ca + "n"])
        cn, cns = "ca%d" % (t + 1), "cas%d" % (t + 1)
        CL = ["clst0", "clst1", ca + "n"]
        pick("c", cn, G * rank, G, ca, 0, 256, "clst", 0, CL + [ca], [cn])
        pick("s", cns, G * rank, G, cas, 0, 256, "clst", 0, CL + [cas], [cns])
        if last:
            dma("y", T.oc[:, :], T[cn][:, own].bitcast(dt.uint8), [cn], [], "st")
            for k in range(4):
                dma("y" if k == 3 else "s", T.osc[4 * k:4 * k + 4, :], T[cns][32 * k:32 * k + 4, own], [cns], [], "st")
            numbers3()
        else:
            remote([many(T[cn][:, own].bitcast(dt.uint8), T[cn][:, own].bitcast(dt.uint8), "arc%d" % (t + 1))], [cn])
            remote([many(T[cns][:, own], T[cns][:, own], "arc%d" % (t + 1))], [cns])
            quant("xq", "xs", 192 * t + 192, 192 * t + 384, "xt", 768 * t + 768, ["xt%d" % (t + 1)], ["xq%d" % (t + 1)])
            outputs()
            numbers1()
            zero_block(t + 1)
            numbers2()
            numbers3()
            arrive("arc%d" % (t + 1), n_cen, [cn, cns])
            if t == 0:
                await_("y", writers["ca1"])
                dma("y", T.xt[:, 1536:2304], T.x[:, 1536:2304], [], ["xt2"], "ldx2")
    for k in cnt:
        if know["p"].get(k, 0) < cnt[k]:
            g.wait_ge(T.sem[k], cnt[k])
